import numpy as np
import ml_dtypes


def mxq(x, axis, fmt="e4m3"):
    dtype, down = {"e4m3": (ml_dtypes.float8_e4m3fn, 7), "e5m2": (ml_dtypes.float8_e5m2, 14)}[fmt]
    v = np.moveaxis(np.asarray(x, np.float32).astype(ml_dtypes.bfloat16).astype(np.float64), axis, -1)
    blocks = v.reshape(v.shape[:-1] + (-1, 32))
    amax = np.abs(blocks).max(-1, keepdims=True)
    byte = np.maximum(np.where(amax > 0, np.frexp(amax)[1] - 1 + 127, 0) - down, 1)
    scale = np.exp2(byte - 127.0)
    codes = (blocks / scale).astype(np.float32).astype(dtype).astype(np.float64)
    return np.moveaxis((codes * scale).reshape(v.shape), -1, axis)


WIDE = False


def mx_kscale(k):
    if not WIDE:
        return np.ones(k)
    levels = np.array([30, -30])
    if k % 512:
        return np.exp2(np.random.permutation(np.resize(levels, k // 32))).repeat(32)
    a = np.empty((k // 512, 16))
    for p in range(k // 512):
        a[p, :8] = np.random.permutation(np.resize(levels, 8))
        for g in range(8):
            far = levels[np.abs(levels - a[p, g]) >= 10]
            a[p, g + 8] = far[np.random.randint(len(far))]
    return np.exp2(a.ravel()).repeat(32)


def f64(x):
    return np.asarray(x).astype(np.float64)


K, M, T = 2048, 512, 1536


def setup_inputs():
    n = np.random.standard_normal
    s1 = mx_kscale(K)[:, None]
    s2 = mx_kscale(K)[:, None]
    return {
        "w": (n((K, M)) / np.sqrt(K) * s1).astype(np.float32),
        "xd": (n((K, T)) / s1).astype(np.float32),
        "wd": (n((K, M)) / np.sqrt(K) * s2).astype(np.float32),
        "x": (n((K, T)) / s2).astype(np.float32),
        "b": (0.3 * n(512)).astype(np.float32),
    }


def reference(w, xd, wd, x, b):
    w_ = mxq(f64(w), 0, "e4m3")
    xd_ = mxq(f64(xd), 0, "e5m2")
    wd_ = mxq(f64(wd), 0, "e5m2")
    x_ = mxq(f64(x), 0, "e4m3")
    y = w_.T @ xd_ + wd_.T @ x_
    return y + f64(b)[:, None]

@@ -1,0 +1,198 @@
+from contextlib import ExitStack
+
+import concourse.mybir as mybir
+from concourse.masks import make_identity
+
+K, M, T = 2048, 512, 1536
+FLOPS = 2 * 2 * K * M * T
+
+F32 = mybir.dt.float32
+BF16 = mybir.dt.bfloat16
+U32 = mybir.dt.uint32
+U8 = mybir.dt.uint8
+E4M3 = mybir.dt.float8_e4m3fn_x4
+E5M2 = mybir.dt.float8_e5m2_x4
+
+P = 128
+PACK = 4
+K_PASS = P * PACK
+COLS = 512
+HALF = COLS // 2
+PASSES_PER_PRODUCT = K // K_PASS
+PASSES = 2 * PASSES_PER_PRODUCT
+M_TILES = M // P
+WHOLE = 5
+
+
+def tile_mix_jvp_fm_bias_kernel(tc, w, xd, wd, x, b, out):
+    nc = tc.nc
+    weights = [(w, E4M3), (wd, E5M2)]
+    acts = [(xd, E5M2), (x, E4M3)]
+
+    with ExitStack() as ctx:
+        raw_pool = ctx.enter_context(tc.tile_pool(name="raw", bufs=5))
+        bf_pool = ctx.enter_context(tc.tile_pool(name="grouped", bufs=4))
+        ring = ctx.enter_context(tc.tile_pool(name="ring", bufs=4))
+        keep = ctx.enter_context(tc.tile_pool(name="keep", bufs=1))
+        psum = ctx.enter_context(tc.psum_pool(name="psum", bufs=1))
+        ctx.enter_context(tc.manual_schedule())
+
+        quantised = {}
+        acc = {}
+        res = {}
+
+        def load_weights(g):
+            src = weights[g // PASSES_PER_PRODUCT][0]
+            k0 = (g % PASSES_PER_PRODUCT) * K_PASS
+            raw = raw_pool.tile([P, 2, PACK, COLS], F32, name="raw", tag="raw")
+            nc.sync.dma_start(
+                out=raw[:],
+                in_=src[k0 : k0 + 2 * K_PASS, :].rearrange("(g p j) c -> p g j c", g=2, j=PACK),
+            )
+            return [(("w", g + i), raw[:, i, :, :]) for i in range(2)]
+
+        def load_acts(g, t0, t1):
+            src = acts[g // PASSES_PER_PRODUCT][0]
+            k0 = (g % PASSES_PER_PRODUCT) * K_PASS
+            raw = raw_pool.tile([P, PACK, (t1 - t0) * COLS], F32, name="raw", tag="raw")
+            nc.sync.dma_start(
+                out=raw[:],
+                in_=src[k0 : k0 + K_PASS, t0 * COLS : t1 * COLS].rearrange("(p j) c -> p j c", j=PACK),
+            )
+            return [(("x", g, t), raw[:, :, (t - t0) * COLS : (t - t0 + 1) * COLS]) for t in range(t0, t1)]
+
+        def interleave(rows):
+            grouped = bf_pool.tile([P, COLS, PACK], BF16, name="grouped", tag="grouped", align_bytes=64)
+            nc.scalar.copy(out=grouped[:, :HALF, :], in_=rows[:, :, :HALF].rearrange("p j c -> p c j"))
+            nc.vector.tensor_copy(out=grouped[:, HALF:, :], in_=rows[:, :, HALF:].rearrange("p j c -> p c j"))
+            return grouped
+
+        def quantise(key, grouped, spans):
+            fmt = (weights if key[0] == "w" else acts)[key[1] // PASSES_PER_PRODUCT][1]
+            if key[0] == "x" and key[2] < 2:
+                codes = ring.tile([P, COLS], U32, name="codes", tag="codes", align_bytes=64)
+                scales = ring.tile([P, COLS], U8, name="scales", tag="scales", align_bytes=64)
+            else:
+                label = "%s%d" % (key[0], key[1])
+                codes = keep.tile([P, COLS], U32, name="codes_" + label, tag="codes_" + label, align_bytes=64)
+                scales = keep.tile([P, COLS], U8, name="scales_" + label, tag="scales_" + label, align_bytes=64)
+            for c0, c1 in spans:
+                nc.vector.quantize_mx(
+                    out=codes[:, c0:c1].bitcast(fmt),
+                    scales=scales[:, c0:c1],
+                    in_=grouped[:, c0:c1, :].rearrange("p c j -> p (c j)"),
+                )
+            quantised[key] = (codes, scales, fmt)
+
+        def prepare(chunks):
+            waiting = None
+            for key, rows in chunks:
+                grouped = interleave(rows)
+                if waiting is not None:
+                    quantise(waiting[0], waiting[1], [(0, COLS)])
+                waiting = (key, grouped)
+            quantise(waiting[0], waiting[1], [(HALF, COLS), (0, HALF)])
+
+        def open_banks(t):
+            for m in range(M_TILES):
+                bank = "bank%d" % (M_TILES * (t % 2) + m)
+                acc[t, m] = psum.tile([P, COLS], F32, name=bank, tag=bank)
+
+        def multiply(g, t, m):
+            w_codes, w_scales, w_fmt = quantised["w", g]
+            x_codes, x_scales, x_fmt = quantised["x", g, t]
+            cols = slice(m * P, (m + 1) * P)
+            nc.tensor.matmul_mx(
+                out=acc[t, m][:],
+                lhsT=w_codes[:, cols].bitcast(w_fmt),
+                lhsT_scale=w_scales[:, cols],
+                rhs=x_codes[:].bitcast(x_fmt),
+                rhs_scale=x_scales[:],
+                start=(g == 0),
+                stop=(g == PASSES - 1),
+            )
+
+        def multiply_all(g, t):
+            for m in range(M_TILES):
+                multiply(g, t, m)
+
+        def drain_on_scalar(t, m):
+            nc.scalar.activation(
+                out=res[t][:, m, :],
+                in_=acc[t, m][:],
+                func=mybir.ActivationFunctionType.Identity,
+                bias=bias[:, m : m + 1],
+            )
+
+        def drain_on_vector(t, m):
+            nc.vector.tensor_scalar(
+                out=res[t][:, m, :],
+                in0=acc[t, m][:],
+                scalar1=bias[:, m : m + 1],
+                scalar2=None,
+                op0=mybir.AluOpType.add,
+            )
+
+        def store(t, m0, m1):
+            nc.sync.dma_start(
+                out=out[m0 * P : m1 * P, t * COLS : (t + 1) * COLS].rearrange("(m p) c -> p m c", p=P),
+                in_=res[t][:, m0:m1, :],
+            )
+
+        first = load_weights(0)
+
+        b_rows = keep.tile([P, P], F32, name="b_rows", tag="b_rows")
+        ident = keep.tile([P, P], F32, name="ident", tag="ident")
+        bias = keep.tile([P, M_TILES], F32, name="bias", tag="bias")
+        nc.vector.memset(b_rows[:], 0.0)
+        nc.sync.dma_start(out=b_rows[:M_TILES, :], in_=b.rearrange("(m p) -> m p", p=P))
+        make_identity(nc, ident[:])
+        prepare(first)
+        b_cols = psum.tile([P, P], F32, name="b_cols", tag="bank7")
+        nc.tensor.transpose(b_cols[:], b_rows[:], ident[:])
+        nc.scalar.copy(out=bias[:], in_=b_cols[:, :M_TILES])
+        for t in range(3):
+            res[t] = keep.tile([P, M_TILES, COLS], F32, name="res%d" % t, tag="res%d" % t)
+
+        open_banks(0)
+        open_banks(1)
+        for g in range(WHOLE):
+            if g > 0 and g % 2 == 0:
+                prepare(load_weights(g))
+            prepare(load_acts(g, 0, 3))
+            multiply_all(g, 0)
+            multiply_all(g, 1)
+        prepare(load_weights(6))
+
+        for g in range(WHOLE, PASSES):
+            prepare(load_acts(g, 0, 1))
+            multiply_all(g, 0)
+        for m in range(M_TILES):
+            (drain_on_scalar if m % 2 == 0 else drain_on_vector)(0, m)
+
+        open_banks(2)
+        for m in range(M_TILES):
+            for g in range(WHOLE):
+                multiply(g, 2, m)
+
+        prepare(load_acts(5, 1, 3))
+        multiply_all(5, 1)
+        for g in (6, 7):
+            prepare(load_acts(g, 1, 2))
+            multiply_all(g, 1)
+        multiply_all(5, 2)
+        drain_on_scalar(1, 0)
+        drain_on_vector(1, 1)
+        for g in (6, 7):
+            prepare(load_acts(g, 2, 3))
+            multiply_all(g, 2)
+        drain_on_scalar(1, 2)
+        drain_on_scalar(1, 3)
+        for m in range(M_TILES):
+            (drain_on_vector if m % 2 == 0 else drain_on_scalar)(2, m)
+
+        store(0, 0, M_TILES)
+        store(1, 0, 2)
+        store(1, 2, M_TILES)
+        for m in range(M_TILES):
+            store(2, m, m + 1)

@@ -22,6 +22,7 @@ PASSES_PER_PRODUCT = K // K_PASS
 PASSES = 2 * PASSES_PER_PRODUCT
 M_TILES = M // P
 WHOLE = 5
+SCALAR_COLS = 192
 
 
 def tile_mix_jvp_fm_bias_kernel(tc, w, xd, wd, x, b, out):
@@ -39,17 +40,16 @@ def tile_mix_jvp_fm_bias_kernel(tc, w, xd, wd, x, b, out):
 
         quantised = {}
         acc = {}
-        res = {}
 
-        def load_weights(g):
+        def load_weights(g, count):
             src = weights[g // PASSES_PER_PRODUCT][0]
             k0 = (g % PASSES_PER_PRODUCT) * K_PASS
-            raw = raw_pool.tile([P, 2, PACK, COLS], F32, name="raw", tag="raw")
+            raw = raw_pool.tile([P, count, PACK, COLS], F32, name="raw", tag="raw")
             nc.sync.dma_start(
                 out=raw[:],
-                in_=src[k0 : k0 + 2 * K_PASS, :].rearrange("(g p j) c -> p g j c", g=2, j=PACK),
+                in_=src[k0 : k0 + count * K_PASS, :].rearrange("(g p j) c -> p g j c", g=count, j=PACK),
             )
-            return [(("w", g + i), raw[:, i, :, :]) for i in range(2)]
+            return [(("w", g + i), raw[:, i, :, :]) for i in range(count)]
 
         def load_acts(g, t0, t1):
             src = acts[g // PASSES_PER_PRODUCT][0]
@@ -63,8 +63,9 @@ def tile_mix_jvp_fm_bias_kernel(tc, w, xd, wd, x, b, out):
 
         def interleave(rows):
             grouped = bf_pool.tile([P, COLS, PACK], BF16, name="grouped", tag="grouped", align_bytes=64)
-            nc.scalar.copy(out=grouped[:, :HALF, :], in_=rows[:, :, :HALF].rearrange("p j c -> p c j"))
-            nc.vector.tensor_copy(out=grouped[:, HALF:, :], in_=rows[:, :, HALF:].rearrange("p j c -> p c j"))
+            nc.scalar.copy(out=grouped[:, :SCALAR_COLS, :], in_=rows[:, :, :SCALAR_COLS].rearrange("p j c -> p c j"))
+            for c0, c1 in ((HALF, COLS), (SCALAR_COLS, HALF)):
+                nc.vector.tensor_copy(out=grouped[:, c0:c1, :], in_=rows[:, :, c0:c1].rearrange("p j c -> p c j"))
             return grouped
 
         def quantise(key, grouped, spans):
@@ -118,7 +119,7 @@ def tile_mix_jvp_fm_bias_kernel(tc, w, xd, wd, x, b, out):
 
         def drain_on_scalar(t, m):
             nc.scalar.activation(
-                out=res[t][:, m, :],
+                out=res[:, m, t * COLS : (t + 1) * COLS],
                 in_=acc[t, m][:],
                 func=mybir.ActivationFunctionType.Identity,
                 bias=bias[:, m : m + 1],
@@ -126,20 +127,20 @@ def tile_mix_jvp_fm_bias_kernel(tc, w, xd, wd, x, b, out):
 
         def drain_on_vector(t, m):
             nc.vector.tensor_scalar(
-                out=res[t][:, m, :],
+                out=res[:, m, t * COLS : (t + 1) * COLS],
                 in0=acc[t, m][:],
                 scalar1=bias[:, m : m + 1],
                 scalar2=None,
                 op0=mybir.AluOpType.add,
             )
 
-        def store(t, m0, m1):
+        def store(t0, t1, m0, m1):
             nc.sync.dma_start(
-                out=out[m0 * P : m1 * P, t * COLS : (t + 1) * COLS].rearrange("(m p) c -> p m c", p=P),
-                in_=res[t][:, m0:m1, :],
+                out=out[m0 * P : m1 * P, t0 * COLS : t1 * COLS].rearrange("(m p) c -> p m c", p=P),
+                in_=res[:, m0:m1, t0 * COLS : t1 * COLS],
             )
 
-        first = load_weights(0)
+        first = load_weights(0, 2)
 
         b_rows = keep.tile([P, P], F32, name="b_rows", tag="b_rows")
         ident = keep.tile([P, P], F32, name="ident", tag="ident")
@@ -151,48 +152,48 @@ def tile_mix_jvp_fm_bias_kernel(tc, w, xd, wd, x, b, out):
         b_cols = psum.tile([P, P], F32, name="b_cols", tag="bank7")
         nc.tensor.transpose(b_cols[:], b_rows[:], ident[:])
         nc.scalar.copy(out=bias[:], in_=b_cols[:, :M_TILES])
-        for t in range(3):
-            res[t] = keep.tile([P, M_TILES, COLS], F32, name="res%d" % t, tag="res%d" % t)
+        res = keep.tile([P, M_TILES, T], F32, name="res", tag="res")
+
+        def drain_all(t):
+            for m in range(M_TILES):
+                (drain_on_scalar if m % 2 == 0 else drain_on_vector)(t, m)
 
         open_banks(0)
         open_banks(1)
         for g in range(WHOLE):
             if g > 0 and g % 2 == 0:
-                prepare(load_weights(g))
+                prepare(load_weights(g, 2))
             prepare(load_acts(g, 0, 3))
             multiply_all(g, 0)
             multiply_all(g, 1)
-        prepare(load_weights(6))
 
-        for g in range(WHOLE, PASSES):
-            prepare(load_acts(g, 0, 1))
+        prepare(load_weights(6, 1))
+        for g in (5, 6):
+            prepare(load_acts(g, 0, 2))
             multiply_all(g, 0)
-        for m in range(M_TILES):
-            (drain_on_scalar if m % 2 == 0 else drain_on_vector)(0, m)
+            multiply_all(g, 1)
+        prepare(load_weights(7, 1))
+        prepare(load_acts(7, 0, 1))
+        multiply_all(7, 0)
+        drain_all(0)
 
         open_banks(2)
+        prepare(load_acts(7, 1, 2))
         for m in range(M_TILES):
+            if m == 2:
+                multiply_all(7, 1)
             for g in range(WHOLE):
                 multiply(g, 2, m)
 
-        prepare(load_acts(5, 1, 3))
-        multiply_all(5, 1)
-        for g in (6, 7):
-            prepare(load_acts(g, 1, 2))
-            multiply_all(g, 1)
+        prepare(load_acts(5, 2, 3))
+        drain_all(1)
         multiply_all(5, 2)
-        drain_on_scalar(1, 0)
-        drain_on_vector(1, 1)
-        for g in (6, 7):
-            prepare(load_acts(g, 2, 3))
-            multiply_all(g, 2)
-        drain_on_scalar(1, 2)
-        drain_on_scalar(1, 3)
-        for m in range(M_TILES):
-            (drain_on_vector if m % 2 == 0 else drain_on_scalar)(2, m)
+        prepare(load_acts(6, 2, 3))
+        prepare(load_acts(7, 2, 3))
+        for g, m in ((6, 0), (6, 1), (7, 0), (7, 1), (6, 2), (7, 2), (6, 3), (7, 3)):
+            multiply(g, 2, m)
+        drain_all(2)
 
-        store(0, 0, M_TILES)
-        store(1, 0, 2)
-        store(1, 2, M_TILES)
+        store(0, 2, 0, M_TILES)
         for m in range(M_TILES):
-            store(2, m, m + 1)
+            store(2, 3, m, m + 1)

@@ -23,6 +23,7 @@ PASSES = 2 * PASSES_PER_PRODUCT
 M_TILES = M // P
 WHOLE = 5
 SCALAR_COLS = 192
+RUN = 4
 
 
 def tile_mix_jvp_fm_bias_kernel(tc, w, xd, wd, x, b, out):
@@ -63,9 +64,11 @@ def tile_mix_jvp_fm_bias_kernel(tc, w, xd, wd, x, b, out):
 
         def interleave(rows):
             grouped = bf_pool.tile([P, COLS, PACK], BF16, name="grouped", tag="grouped", align_bytes=64)
-            nc.scalar.copy(out=grouped[:, :SCALAR_COLS, :], in_=rows[:, :, :SCALAR_COLS].rearrange("p j c -> p c j"))
+            dst = grouped[:].rearrange("p (c i) j -> p c j i", i=RUN)
+            src = rows.rearrange("p j (c i) -> p c j i", i=RUN)
+            nc.scalar.copy(out=dst[:, : SCALAR_COLS // RUN], in_=src[:, : SCALAR_COLS // RUN])
             for c0, c1 in ((HALF, COLS), (SCALAR_COLS, HALF)):
-                nc.vector.tensor_copy(out=grouped[:, c0:c1, :], in_=rows[:, :, c0:c1].rearrange("p j c -> p c j"))
+                nc.vector.tensor_copy(out=dst[:, c0 // RUN : c1 // RUN], in_=src[:, c0 // RUN : c1 // RUN])
             return grouped
 
         def quantise(key, grouped, spans):
@@ -187,13 +190,17 @@ def tile_mix_jvp_fm_bias_kernel(tc, w, xd, wd, x, b, out):
 
         prepare(load_acts(5, 2, 3))
         drain_all(1)
-        multiply_all(5, 2)
         prepare(load_acts(6, 2, 3))
         prepare(load_acts(7, 2, 3))
-        for g, m in ((6, 0), (6, 1), (7, 0), (7, 1), (6, 2), (7, 2), (6, 3), (7, 3)):
-            multiply(g, 2, m)
+        for g in (5, 6, 7):
+            for m in (0, 1):
+                multiply(g, 2, m)
+        for m in (2, 3):
+            for g in (5, 6, 7):
+                multiply(g, 2, m)
         drain_all(2)
 
-        store(0, 2, 0, M_TILES)
+        store(0, 2, 0, 2)
+        store(0, 2, 2, M_TILES)
         for m in range(M_TILES):
             store(2, 3, m, m + 1)

@@ -21,9 +21,9 @@ HALF = COLS // 2
 PASSES_PER_PRODUCT = K // K_PASS
 PASSES = 2 * PASSES_PER_PRODUCT
 M_TILES = M // P
-WHOLE = 5
-SCALAR_COLS = 192
+EARLY = 5
 RUN = 4
+LONE_SCALAR_COLS = 192
 
 
 def tile_mix_jvp_fm_bias_kernel(tc, w, xd, wd, x, b, out):
@@ -41,6 +41,9 @@ def tile_mix_jvp_fm_bias_kernel(tc, w, xd, wd, x, b, out):
 
         quantised = {}
         acc = {}
+
+        def late_tile(g):
+            return 1 if g < EARLY else 2
 
         def load_weights(g, count):
             src = weights[g // PASSES_PER_PRODUCT][0]
@@ -62,18 +65,20 @@ def tile_mix_jvp_fm_bias_kernel(tc, w, xd, wd, x, b, out):
             )
             return [(("x", g, t), raw[:, :, (t - t0) * COLS : (t - t0 + 1) * COLS]) for t in range(t0, t1)]
 
-        def interleave(rows):
+        def interleave(rows, scalar_cols):
             grouped = bf_pool.tile([P, COLS, PACK], BF16, name="grouped", tag="grouped", align_bytes=64)
             dst = grouped[:].rearrange("p (c i) j -> p c j i", i=RUN)
             src = rows.rearrange("p j (c i) -> p c j i", i=RUN)
-            nc.scalar.copy(out=dst[:, : SCALAR_COLS // RUN], in_=src[:, : SCALAR_COLS // RUN])
-            for c0, c1 in ((HALF, COLS), (SCALAR_COLS, HALF)):
-                nc.vector.tensor_copy(out=dst[:, c0 // RUN : c1 // RUN], in_=src[:, c0 // RUN : c1 // RUN])
+            if scalar_cols > 0:
+                nc.scalar.copy(out=dst[:, : scalar_cols // RUN], in_=src[:, : scalar_cols // RUN])
+            for c0, c1 in ((HALF, COLS), (scalar_cols, HALF)):
+                if c0 < c1:
+                    nc.vector.tensor_copy(out=dst[:, c0 // RUN : c1 // RUN], in_=src[:, c0 // RUN : c1 // RUN])
             return grouped
 
         def quantise(key, grouped, spans):
             fmt = (weights if key[0] == "w" else acts)[key[1] // PASSES_PER_PRODUCT][1]
-            if key[0] == "x" and key[2] < 2:
+            if key[0] == "x" and key[2] != late_tile(key[1]):
                 codes = ring.tile([P, COLS], U32, name="codes", tag="codes", align_bytes=64)
                 scales = ring.tile([P, COLS], U8, name="scales", tag="scales", align_bytes=64)
             else:
@@ -88,19 +93,18 @@ def tile_mix_jvp_fm_bias_kernel(tc, w, xd, wd, x, b, out):
                 )
             quantised[key] = (codes, scales, fmt)
 
-        def prepare(chunks):
+        def prepare(chunks, scalar_cols=HALF):
             waiting = None
             for key, rows in chunks:
-                grouped = interleave(rows)
+                grouped = interleave(rows, scalar_cols)
                 if waiting is not None:
                     quantise(waiting[0], waiting[1], [(0, COLS)])
                 waiting = (key, grouped)
             quantise(waiting[0], waiting[1], [(HALF, COLS), (0, HALF)])
 
-        def open_banks(t):
-            for m in range(M_TILES):
-                bank = "bank%d" % (M_TILES * (t % 2) + m)
-                acc[t, m] = psum.tile([P, COLS], F32, name=bank, tag=bank)
+        def open_bank(t, m, half):
+            bank = "bank%d" % (M_TILES * half + m)
+            acc[t, m] = psum.tile([P, COLS], F32, name=bank, tag=bank)
 
         def multiply(g, t, m):
             w_codes, w_scales, w_fmt = quantised["w", g]
@@ -112,8 +116,8 @@ def tile_mix_jvp_fm_bias_kernel(tc, w, xd, wd, x, b, out):
                 lhsT_scale=w_scales[:, cols],
                 rhs=x_codes[:].bitcast(x_fmt),
                 rhs_scale=x_scales[:],
-                start=(g == 0),
-                stop=(g == PASSES - 1),
+                start=(g == 0 or (t == 2 and g == EARLY)),
+                stop=(g == PASSES - 1 or (t == 2 and g == EARLY - 1)),
             )
 
         def multiply_all(g, t):
@@ -128,13 +132,20 @@ def tile_mix_jvp_fm_bias_kernel(tc, w, xd, wd, x, b, out):
                 bias=bias[:, m : m + 1],
             )
 
-        def drain_on_vector(t, m):
-            nc.vector.tensor_scalar(
-                out=res[:, m, t * COLS : (t + 1) * COLS],
-                in0=acc[t, m][:],
-                scalar1=bias[:, m : m + 1],
-                scalar2=None,
-                op0=mybir.AluOpType.add,
+        def drain_partial(m):
+            nc.scalar.activation(
+                out=partial[:, m, :],
+                in_=acc[2, m][:],
+                func=mybir.ActivationFunctionType.Identity,
+                bias=bias[:, m : m + 1],
+            )
+
+        def drain_onto_partial(m):
+            nc.vector.tensor_tensor(
+                out=res[:, m, 2 * COLS :],
+                in0=acc[2, m][:],
+                in1=partial[:, m, :],
+                op=mybir.AluOpType.add,
             )
 
         def store(t0, t1, m0, m1):
@@ -156,51 +167,53 @@ def tile_mix_jvp_fm_bias_kernel(tc, w, xd, wd, x, b, out):
         nc.tensor.transpose(b_cols[:], b_rows[:], ident[:])
         nc.scalar.copy(out=bias[:], in_=b_cols[:, :M_TILES])
         res = keep.tile([P, M_TILES, T], F32, name="res", tag="res")
+        partial = keep.tile([P, M_TILES, COLS], F32, name="partial", tag="partial")
 
-        def drain_all(t):
-            for m in range(M_TILES):
-                (drain_on_scalar if m % 2 == 0 else drain_on_vector)(t, m)
-
-        open_banks(0)
-        open_banks(1)
-        for g in range(WHOLE):
+        for m in range(M_TILES):
+            open_bank(0, m, 0)
+            open_bank(2, m, 1)
+        for g in range(EARLY):
             if g > 0 and g % 2 == 0:
                 prepare(load_weights(g, 2))
-            prepare(load_acts(g, 0, 3))
+            tiles = load_acts(g, 0, 3)
+            prepare([tiles[2], tiles[0], tiles[1]])
+            multiply_all(g, 2)
             multiply_all(g, 0)
-            multiply_all(g, 1)
 
-        prepare(load_weights(6, 1))
-        for g in (5, 6):
-            prepare(load_acts(g, 0, 2))
-            multiply_all(g, 0)
-            multiply_all(g, 1)
-        prepare(load_weights(7, 1))
-        prepare(load_acts(7, 0, 1))
+        for m in range(M_TILES):
+            drain_partial(m)
+            open_bank(1, m, 1)
+            for g in range(EARLY):
+                multiply(g, 1, m)
+
+        prepare(load_acts(5, 0, 3))
+        multiply_all(5, 0)
+        multiply_all(5, 1)
+        tiles = load_acts(6, 0, 3)
+        prepare(tiles[:2] + load_weights(6, 1) + tiles[2:])
+        multiply_all(6, 0)
+        multiply_all(6, 1)
+        prepare(load_weights(7, 1), LONE_SCALAR_COLS)
+        prepare(load_acts(7, 0, 1), LONE_SCALAR_COLS)
         multiply_all(7, 0)
-        drain_all(0)
+        for m in range(M_TILES):
+            drain_on_scalar(0, m)
 
-        open_banks(2)
-        prepare(load_acts(7, 1, 2))
+        prepare(load_acts(7, 1, 2), 0)
         for m in range(M_TILES):
             if m == 2:
                 multiply_all(7, 1)
-            for g in range(WHOLE):
+            open_bank(2, m, 0)
+            for g in range(EARLY, PASSES - 1):
                 multiply(g, 2, m)
-
-        prepare(load_acts(5, 2, 3))
-        drain_all(1)
-        prepare(load_acts(6, 2, 3))
-        prepare(load_acts(7, 2, 3))
-        for g in (5, 6, 7):
-            for m in (0, 1):
-                multiply(g, 2, m)
-        for m in (2, 3):
-            for g in (5, 6, 7):
-                multiply(g, 2, m)
-        drain_all(2)
-
-        store(0, 2, 0, 2)
-        store(0, 2, 2, M_TILES)
         for m in range(M_TILES):
-            store(2, 3, m, m + 1)
+            drain_on_scalar(1, m)
+
+        prepare(load_acts(7, 2, 3), 0)
+        multiply_all(7, 2)
+        for m in range(M_TILES):
+            drain_onto_partial(m)
+
+        for t in range(3):
+            for m in range(M_TILES):
+                store(t, t + 1, m, m + 1)

@@ -21,7 +21,7 @@ HALF = COLS // 2
 PASSES_PER_PRODUCT = K // K_PASS
 PASSES = 2 * PASSES_PER_PRODUCT
 M_TILES = M // P
-EARLY = 5
+EARLY = 6
 RUN = 4
 LONE_SCALAR_COLS = 192
 
@@ -32,8 +32,10 @@ def tile_mix_jvp_fm_bias_kernel(tc, w, xd, wd, x, b, out):
     acts = [(xd, E5M2), (x, E4M3)]
 
     with ExitStack() as ctx:
-        raw_pool = ctx.enter_context(tc.tile_pool(name="raw", bufs=5))
+        raw_pool = ctx.enter_context(tc.tile_pool(name="raw", bufs=4))
+        w_pool = ctx.enter_context(tc.tile_pool(name="w_raw", bufs=2))
         bf_pool = ctx.enter_context(tc.tile_pool(name="grouped", bufs=4))
+        span_pool = ctx.enter_context(tc.tile_pool(name="spans", bufs=6))
         ring = ctx.enter_context(tc.tile_pool(name="ring", bufs=4))
         keep = ctx.enter_context(tc.tile_pool(name="keep", bufs=1))
         psum = ctx.enter_context(tc.psum_pool(name="psum", bufs=1))
@@ -48,7 +50,7 @@ def tile_mix_jvp_fm_bias_kernel(tc, w, xd, wd, x, b, out):
         def load_weights(g, count):
             src = weights[g // PASSES_PER_PRODUCT][0]
             k0 = (g % PASSES_PER_PRODUCT) * K_PASS
-            raw = raw_pool.tile([P, count, PACK, COLS], F32, name="raw", tag="raw")
+            raw = w_pool.tile([P, count, PACK, COLS], F32, name="w_raw", tag="w_raw")
             nc.sync.dma_start(
                 out=raw[:],
                 in_=src[k0 : k0 + count * K_PASS, :].rearrange("(g p j) c -> p g j c", g=count, j=PACK),
@@ -101,6 +103,38 @@ def tile_mix_jvp_fm_bias_kernel(tc, w, xd, wd, x, b, out):
                     quantise(waiting[0], waiting[1], [(0, COLS)])
                 waiting = (key, grouped)
             quantise(waiting[0], waiting[1], [(HALF, COLS), (0, HALF)])
+
+        def load_last(c0, c1):
+            raw = raw_pool.tile([P, PACK, c1 - c0], F32, name="raw", tag="raw")
+            nc.sync.dma_start(
+                out=raw[:],
+                in_=x[K - K_PASS :, c0:c1].rearrange("(p j) c -> p j c", j=PACK),
+            )
+            return raw
+
+        def new_codes(key, fmt):
+            label = "%s7_%d" % (key[0], key[-1])
+            codes = keep.tile([P, COLS], U32, name="codes_" + label, tag="codes_" + label, align_bytes=64)
+            scales = keep.tile([P, COLS], U8, name="scales_" + label, tag="scales_" + label, align_bytes=64)
+            quantised[key] = (codes, scales, fmt)
+
+        def copy_span(engine_copy, rows):
+            width = rows.shape[2]
+            span = span_pool.tile([P, width, PACK], BF16, name="span", tag="span", align_bytes=64)
+            engine_copy(
+                out=span[:].rearrange("p (c i) j -> p c j i", i=RUN),
+                in_=rows.rearrange("p j (c i) -> p c j i", i=RUN),
+            )
+            return span
+
+        def quantise_span(key, c0, span):
+            codes, scales, fmt = quantised[key]
+            c1 = c0 + span.shape[1]
+            nc.vector.quantize_mx(
+                out=codes[:, c0:c1].bitcast(fmt),
+                scales=scales[:, c0:c1],
+                in_=span[:].rearrange("p c j -> p (c j)"),
+            )
 
         def open_bank(t, m, half):
             bank = "bank%d" % (M_TILES * half + m)
@@ -186,20 +220,36 @@ def tile_mix_jvp_fm_bias_kernel(tc, w, xd, wd, x, b, out):
             for g in range(EARLY):
                 multiply(g, 1, m)
 
-        prepare(load_acts(5, 0, 3))
-        multiply_all(5, 0)
-        multiply_all(5, 1)
         tiles = load_acts(6, 0, 3)
         prepare(tiles[:2] + load_weights(6, 1) + tiles[2:])
         multiply_all(6, 0)
         multiply_all(6, 1)
-        prepare(load_weights(7, 1), LONE_SCALAR_COLS)
-        prepare(load_acts(7, 0, 1), LONE_SCALAR_COLS)
+
+        for t in range(3):
+            new_codes(("x", 7, t), E4M3)
+        raw = load_last(0, 640)
+        spans = []
+        for i in range(5):
+            spans.append(copy_span(nc.vector.tensor_copy if i % 2 == 0 else nc.scalar.copy, raw[:, :, i * P : (i + 1) * P]))
+        for i in range(len(spans)):
+            quantise_span(("x", 7, i * P // COLS), i * P % COLS, spans[i])
+
+        rows = load_weights(7, 1)[0][1]
+        new_codes(("w", 7), E5M2)
+        spans = []
+        for m in range(M_TILES):
+            spans.append(copy_span(nc.vector.tensor_copy if m % 2 == 0 else nc.scalar.copy, rows[:, :, m * P : (m + 1) * P]))
+        for m in range(M_TILES):
+            quantise_span(("w", 7), m * P, spans[m])
         multiply_all(7, 0)
         for m in range(M_TILES):
             drain_on_scalar(0, m)
 
-        prepare(load_acts(7, 1, 2), 0)
+        raw = load_last(640, 1024)
+        spans = [copy_span(nc.vector.tensor_copy, raw[:, :, i * P : (i + 1) * P]) for i in range(3)]
+        for i in range(len(spans)):
+            quantise_span(("x", 7, (640 + i * P) // COLS), (640 + i * P) % COLS, spans[i])
+
         for m in range(M_TILES):
             if m == 2:
                 multiply_all(7, 1)
@@ -209,7 +259,16 @@ def tile_mix_jvp_fm_bias_kernel(tc, w, xd, wd, x, b, out):
         for m in range(M_TILES):
             drain_on_scalar(1, m)
 
-        prepare(load_acts(7, 2, 3), 0)
+        raw = load_last(1024, 1280)
+        spans = [copy_span(nc.vector.tensor_copy, raw[:, :, i * P : (i + 1) * P]) for i in range(2)]
+        for i in range(len(spans)):
+            quantise_span(("x", 7, (1024 + i * P) // COLS), (1024 + i * P) % COLS, spans[i])
+
+        raw = load_last(1280, 1536)
+        spans = [copy_span(nc.vector.tensor_copy, raw[:, :, i * P : (i + 1) * P]) for i in range(2)]
+        for i in range(len(spans)):
+            quantise_span(("x", 7, (1280 + i * P) // COLS), (1280 + i * P) % COLS, spans[i])
+
         multiply_all(7, 2)
         for m in range(M_TILES):
             drain_onto_partial(m)

@@ -35,7 +35,7 @@ def tile_mix_jvp_fm_bias_kernel(tc, w, xd, wd, x, b, out):
         raw_pool = ctx.enter_context(tc.tile_pool(name="raw", bufs=4))
         w_pool = ctx.enter_context(tc.tile_pool(name="w_raw", bufs=2))
         bf_pool = ctx.enter_context(tc.tile_pool(name="grouped", bufs=4))
-        span_pool = ctx.enter_context(tc.tile_pool(name="spans", bufs=6))
+        span_pool = ctx.enter_context(tc.tile_pool(name="spans", bufs=5))
         ring = ctx.enter_context(tc.tile_pool(name="ring", bufs=4))
         keep = ctx.enter_context(tc.tile_pool(name="keep", bufs=1))
         psum = ctx.enter_context(tc.psum_pool(name="psum", bufs=1))
@@ -50,7 +50,7 @@ def tile_mix_jvp_fm_bias_kernel(tc, w, xd, wd, x, b, out):
         def load_weights(g, count):
             src = weights[g // PASSES_PER_PRODUCT][0]
             k0 = (g % PASSES_PER_PRODUCT) * K_PASS
-            raw = w_pool.tile([P, count, PACK, COLS], F32, name="w_raw", tag="w_raw")
+            raw = w_pool.tile([P, count, PACK, COLS], F32, name="w_raw", tag="w_raw", align_bytes=256)
             nc.sync.dma_start(
                 out=raw[:],
                 in_=src[k0 : k0 + count * K_PASS, :].rearrange("(g p j) c -> p g j c", g=count, j=PACK),
@@ -60,7 +60,7 @@ def tile_mix_jvp_fm_bias_kernel(tc, w, xd, wd, x, b, out):
         def load_acts(g, t0, t1):
             src = acts[g // PASSES_PER_PRODUCT][0]
             k0 = (g % PASSES_PER_PRODUCT) * K_PASS
-            raw = raw_pool.tile([P, PACK, (t1 - t0) * COLS], F32, name="raw", tag="raw")
+            raw = raw_pool.tile([P, PACK, (t1 - t0) * COLS], F32, name="raw", tag="raw", align_bytes=256)
             nc.sync.dma_start(
                 out=raw[:],
                 in_=src[k0 : k0 + K_PASS, t0 * COLS : t1 * COLS].rearrange("(p j) c -> p j c", j=PACK),
@@ -105,7 +105,7 @@ def tile_mix_jvp_fm_bias_kernel(tc, w, xd, wd, x, b, out):
             quantise(waiting[0], waiting[1], [(HALF, COLS), (0, HALF)])
 
         def load_last(c0, c1):
-            raw = raw_pool.tile([P, PACK, c1 - c0], F32, name="raw", tag="raw")
+            raw = raw_pool.tile([P, PACK, c1 - c0], F32, name="raw", tag="raw", align_bytes=256)
             nc.sync.dma_start(
                 out=raw[:],
                 in_=x[K - K_PASS :, c0:c1].rearrange("(p j) c -> p j c", j=PACK),
@@ -200,7 +200,7 @@ def tile_mix_jvp_fm_bias_kernel(tc, w, xd, wd, x, b, out):
         b_cols = psum.tile([P, P], F32, name="b_cols", tag="bank7")
         nc.tensor.transpose(b_cols[:], b_rows[:], ident[:])
         nc.scalar.copy(out=bias[:], in_=b_cols[:, :M_TILES])
-        res = keep.tile([P, M_TILES, T], F32, name="res", tag="res")
+        res = keep.tile([P, M_TILES, T], F32, name="res", tag="res", align_bytes=256)
         partial = keep.tile([P, M_TILES, COLS], F32, name="partial", tag="partial")
 
         for m in range(M_TILES):

@@ -20,10 +20,16 @@ COLS = 512
 HALF = COLS // 2
 PASSES_PER_PRODUCT = K // K_PASS
 PASSES = 2 * PASSES_PER_PRODUCT
+LAST = PASSES - 1
 M_TILES = M // P
-EARLY = 6
+T_TILES = T // COLS
 RUN = 4
-LONE_SCALAR_COLS = 192
+SLOTS = 4
+MX_ALIGN = 64
+DMA_ALIGN = 256
+
+FIRST_GROUP = 6
+PIECES = (0, 640, 1024, 1280, 1536)
 
 
 def tile_mix_jvp_fm_bias_kernel(tc, w, xd, wd, x, b, out):
@@ -32,112 +38,103 @@ def tile_mix_jvp_fm_bias_kernel(tc, w, xd, wd, x, b, out):
     acts = [(xd, E5M2), (x, E4M3)]
 
     with ExitStack() as ctx:
-        raw_pool = ctx.enter_context(tc.tile_pool(name="raw", bufs=4))
-        w_pool = ctx.enter_context(tc.tile_pool(name="w_raw", bufs=2))
-        bf_pool = ctx.enter_context(tc.tile_pool(name="grouped", bufs=4))
-        span_pool = ctx.enter_context(tc.tile_pool(name="spans", bufs=5))
+        stage = ctx.enter_context(tc.tile_pool(name="stage", bufs=1))
+        chunk_pool = ctx.enter_context(tc.tile_pool(name="chunks", bufs=4))
+        span_pool = ctx.enter_context(tc.tile_pool(name="spans", bufs=PIECES[1] // P))
         ring = ctx.enter_context(tc.tile_pool(name="ring", bufs=4))
         keep = ctx.enter_context(tc.tile_pool(name="keep", bufs=1))
         psum = ctx.enter_context(tc.psum_pool(name="psum", bufs=1))
         ctx.enter_context(tc.manual_schedule())
 
+        w_stage = stage.tile([P, SLOTS, PACK * M], F32, name="w_stage", tag="w_stage", align_bytes=DMA_ALIGN)
+        x_stage = stage.tile([P, SLOTS, PACK * T], F32, name="x_stage", tag="x_stage", align_bytes=DMA_ALIGN)
+        res = stage.tile([P, M_TILES, T], F32, name="res", tag="res", align_bytes=DMA_ALIGN)
+
         quantised = {}
         acc = {}
 
-        def late_tile(g):
-            return 1 if g < EARLY else 2
-
-        def load_weights(g, count):
-            src = weights[g // PASSES_PER_PRODUCT][0]
+        def load_passes(staging, operands, g, count):
+            src = operands[g // PASSES_PER_PRODUCT][0]
             k0 = (g % PASSES_PER_PRODUCT) * K_PASS
-            raw = w_pool.tile([P, count, PACK, COLS], F32, name="w_raw", tag="w_raw", align_bytes=256)
             nc.sync.dma_start(
-                out=raw[:],
-                in_=src[k0 : k0 + count * K_PASS, :].rearrange("(g p j) c -> p g j c", g=count, j=PACK),
+                out=staging[:, g % SLOTS : g % SLOTS + count, :],
+                in_=src[k0 : k0 + count * K_PASS, :].rearrange("(g p j) c -> p g (j c)", g=count, j=PACK),
             )
-            return [(("w", g + i), raw[:, i, :, :]) for i in range(count)]
 
-        def load_acts(g, t0, t1):
-            src = acts[g // PASSES_PER_PRODUCT][0]
-            k0 = (g % PASSES_PER_PRODUCT) * K_PASS
-            raw = raw_pool.tile([P, PACK, (t1 - t0) * COLS], F32, name="raw", tag="raw", align_bytes=256)
-            nc.sync.dma_start(
-                out=raw[:],
-                in_=src[k0 : k0 + K_PASS, t0 * COLS : t1 * COLS].rearrange("(p j) c -> p j c", j=PACK),
-            )
-            return [(("x", g, t), raw[:, :, (t - t0) * COLS : (t - t0 + 1) * COLS]) for t in range(t0, t1)]
+        def load_piece(i):
+            c0, c1 = PIECES[i], PIECES[i + 1]
+            rows = x_stage[:, (LAST + i) % SLOTS, : PACK * (c1 - c0)].rearrange("p (j c) -> p j c", j=PACK)
+            nc.sync.dma_start(out=rows, in_=x[K - K_PASS :, c0:c1].rearrange("(p j) c -> p j c", j=PACK))
+            return rows
 
-        def interleave(rows, scalar_cols):
-            grouped = bf_pool.tile([P, COLS, PACK], BF16, name="grouped", tag="grouped", align_bytes=64)
-            dst = grouped[:].rearrange("p (c i) j -> p c j i", i=RUN)
-            src = rows.rearrange("p j (c i) -> p c j i", i=RUN)
-            if scalar_cols > 0:
-                nc.scalar.copy(out=dst[:, : scalar_cols // RUN], in_=src[:, : scalar_cols // RUN])
-            for c0, c1 in ((HALF, COLS), (scalar_cols, HALF)):
-                if c0 < c1:
-                    nc.vector.tensor_copy(out=dst[:, c0 // RUN : c1 // RUN], in_=src[:, c0 // RUN : c1 // RUN])
-            return grouped
+        def w_chunk(g):
+            return ("w", g), w_stage[:, g % SLOTS, :].rearrange("p (j c) -> p j c", j=PACK)
 
-        def quantise(key, grouped, spans):
-            fmt = (weights if key[0] == "w" else acts)[key[1] // PASSES_PER_PRODUCT][1]
-            if key[0] == "x" and key[2] != late_tile(key[1]):
-                codes = ring.tile([P, COLS], U32, name="codes", tag="codes", align_bytes=64)
-                scales = ring.tile([P, COLS], U8, name="scales", tag="scales", align_bytes=64)
+        def x_chunk(g, t):
+            rows = x_stage[:, g % SLOTS, :].rearrange("p (j c) -> p j c", j=PACK)
+            return ("x", g, t), rows[:, :, t * COLS : (t + 1) * COLS]
+
+        def new_codes(key):
+            g = key[1]
+            fmt = (weights if key[0] == "w" else acts)[g // PASSES_PER_PRODUCT][1]
+            waiting_tile = 1 if g < FIRST_GROUP else 2
+            if key[0] == "x" and g < LAST and key[2] != waiting_tile:
+                pool, label = ring, "ring"
             else:
-                label = "%s%d" % (key[0], key[1])
-                codes = keep.tile([P, COLS], U32, name="codes_" + label, tag="codes_" + label, align_bytes=64)
-                scales = keep.tile([P, COLS], U8, name="scales_" + label, tag="scales_" + label, align_bytes=64)
-            for c0, c1 in spans:
-                nc.vector.quantize_mx(
-                    out=codes[:, c0:c1].bitcast(fmt),
-                    scales=scales[:, c0:c1],
-                    in_=grouped[:, c0:c1, :].rearrange("p c j -> p (c j)"),
-                )
+                pool, label = keep, "%s%d_%d" % (key[0], g, key[-1])
+            codes = pool.tile([P, COLS], U32, name="codes_" + label, tag="codes_" + label, align_bytes=MX_ALIGN)
+            scales = pool.tile([P, COLS], U8, name="scales_" + label, tag="scales_" + label, align_bytes=MX_ALIGN)
             quantised[key] = (codes, scales, fmt)
 
-        def prepare(chunks, scalar_cols=HALF):
-            waiting = None
-            for key, rows in chunks:
-                grouped = interleave(rows, scalar_cols)
-                if waiting is not None:
-                    quantise(waiting[0], waiting[1], [(0, COLS)])
-                waiting = (key, grouped)
-            quantise(waiting[0], waiting[1], [(HALF, COLS), (0, HALF)])
-
-        def load_last(c0, c1):
-            raw = raw_pool.tile([P, PACK, c1 - c0], F32, name="raw", tag="raw", align_bytes=256)
-            nc.sync.dma_start(
-                out=raw[:],
-                in_=x[K - K_PASS :, c0:c1].rearrange("(p j) c -> p j c", j=PACK),
-            )
-            return raw
-
-        def new_codes(key, fmt):
-            label = "%s7_%d" % (key[0], key[-1])
-            codes = keep.tile([P, COLS], U32, name="codes_" + label, tag="codes_" + label, align_bytes=64)
-            scales = keep.tile([P, COLS], U8, name="scales_" + label, tag="scales_" + label, align_bytes=64)
-            quantised[key] = (codes, scales, fmt)
-
-        def copy_span(engine_copy, rows):
-            width = rows.shape[2]
-            span = span_pool.tile([P, width, PACK], BF16, name="span", tag="span", align_bytes=64)
-            engine_copy(
-                out=span[:].rearrange("p (c i) j -> p c j i", i=RUN),
+        def round_and_interleave(copy, rounded, rows):
+            copy(
+                out=rounded.rearrange("p (c i) j -> p c j i", i=RUN),
                 in_=rows.rearrange("p j (c i) -> p c j i", i=RUN),
             )
-            return span
 
-        def quantise_span(key, c0, span):
+        def quantise(key, c0, rounded):
             codes, scales, fmt = quantised[key]
-            c1 = c0 + span.shape[1]
+            c1 = c0 + rounded.shape[1]
             nc.vector.quantize_mx(
                 out=codes[:, c0:c1].bitcast(fmt),
                 scales=scales[:, c0:c1],
-                in_=span[:].rearrange("p c j -> p (c j)"),
+                in_=rounded.rearrange("p c j -> p (c j)"),
             )
 
-        def open_bank(t, m, half):
-            bank = "bank%d" % (M_TILES * half + m)
+        def prepare(chunks):
+            waiting = None
+            for key, rows in chunks:
+                rounded = chunk_pool.tile([P, COLS, PACK], BF16, name="chunk", tag="chunk", align_bytes=MX_ALIGN)
+                round_and_interleave(nc.scalar.copy, rounded[:, :HALF, :], rows[:, :, :HALF])
+                round_and_interleave(nc.vector.tensor_copy, rounded[:, HALF:, :], rows[:, :, HALF:])
+                if waiting is not None:
+                    new_codes(waiting[0])
+                    quantise(waiting[0], 0, waiting[1][:])
+                waiting = (key, rounded)
+            new_codes(waiting[0])
+            quantise(waiting[0], HALF, waiting[1][:, HALF:, :])
+            quantise(waiting[0], 0, waiting[1][:, :HALF, :])
+
+        def prepare_spans(rows, c0, key_of_tile, copies):
+            spans = []
+
+            def quantise_span(i):
+                t, c = divmod(c0 + i * P, COLS)
+                quantise(key_of_tile(t), c, spans[i][:])
+
+            for i in range(rows.shape[2] // P):
+                span = span_pool.tile([P, P, PACK], BF16, name="span", tag="span", align_bytes=MX_ALIGN)
+                round_and_interleave(copies[i % len(copies)], span[:], rows[:, :, i * P : (i + 1) * P])
+                spans.append(span)
+                if i > 0:
+                    quantise_span(i - 1)
+            quantise_span(len(spans) - 1)
+
+        def prepare_piece(i, copies):
+            prepare_spans(load_piece(i), PIECES[i], lambda t: ("x", LAST, t), copies)
+
+        def open_bank(t, m, first_bank):
+            bank = "bank%d" % (first_bank + m)
             acc[t, m] = psum.tile([P, COLS], F32, name=bank, tag=bank)
 
         def multiply(g, t, m):
@@ -150,15 +147,15 @@ def tile_mix_jvp_fm_bias_kernel(tc, w, xd, wd, x, b, out):
                 lhsT_scale=w_scales[:, cols],
                 rhs=x_codes[:].bitcast(x_fmt),
                 rhs_scale=x_scales[:],
-                start=(g == 0 or (t == 2 and g == EARLY)),
-                stop=(g == PASSES - 1 or (t == 2 and g == EARLY - 1)),
+                start=(g == 0 or (t == 2 and g == FIRST_GROUP)),
+                stop=(g == LAST or (t == 2 and g == FIRST_GROUP - 1)),
             )
 
         def multiply_all(g, t):
             for m in range(M_TILES):
                 multiply(g, t, m)
 
-        def drain_on_scalar(t, m):
+        def drain_with_bias(t, m):
             nc.scalar.activation(
                 out=res[:, m, t * COLS : (t + 1) * COLS],
                 in_=acc[t, m][:],
@@ -166,29 +163,20 @@ def tile_mix_jvp_fm_bias_kernel(tc, w, xd, wd, x, b, out):
                 bias=bias[:, m : m + 1],
             )
 
-        def drain_partial(m):
-            nc.scalar.activation(
-                out=partial[:, m, :],
-                in_=acc[2, m][:],
-                func=mybir.ActivationFunctionType.Identity,
-                bias=bias[:, m : m + 1],
-            )
+        def drain_onto_first_group(m):
+            cols = res[:, m, 2 * COLS :]
+            nc.vector.tensor_tensor(out=cols, in0=acc[2, m][:], in1=cols, op=mybir.AluOpType.add)
 
-        def drain_onto_partial(m):
-            nc.vector.tensor_tensor(
-                out=res[:, m, 2 * COLS :],
-                in0=acc[2, m][:],
-                in1=partial[:, m, :],
-                op=mybir.AluOpType.add,
-            )
-
-        def store(t0, t1, m0, m1):
+        def store(t, m0, m1):
             nc.sync.dma_start(
-                out=out[m0 * P : m1 * P, t0 * COLS : t1 * COLS].rearrange("(m p) c -> p m c", p=P),
-                in_=res[:, m0:m1, t0 * COLS : t1 * COLS],
+                out=out[m0 * P : m1 * P, t * COLS : (t + 1) * COLS].rearrange("(m p) c -> p m c", p=P),
+                in_=res[:, m0:m1, t * COLS : (t + 1) * COLS],
             )
 
-        first = load_weights(0, 2)
+        both = [nc.vector.tensor_copy, nc.scalar.copy]
+        vector_alone = [nc.vector.tensor_copy]
+
+        load_passes(w_stage, weights, 0, PASSES_PER_PRODUCT)
 
         b_rows = keep.tile([P, P], F32, name="b_rows", tag="b_rows")
         ident = keep.tile([P, P], F32, name="ident", tag="ident")
@@ -196,83 +184,64 @@ def tile_mix_jvp_fm_bias_kernel(tc, w, xd, wd, x, b, out):
         nc.vector.memset(b_rows[:], 0.0)
         nc.sync.dma_start(out=b_rows[:M_TILES, :], in_=b.rearrange("(m p) -> m p", p=P))
         make_identity(nc, ident[:])
-        prepare(first)
-        b_cols = psum.tile([P, P], F32, name="b_cols", tag="bank7")
+        prepare([w_chunk(g) for g in range(PASSES_PER_PRODUCT)])
+        b_cols = psum.tile([P, P], F32, name="b_cols", tag="bank%d" % (2 * M_TILES - 1))
         nc.tensor.transpose(b_cols[:], b_rows[:], ident[:])
         nc.scalar.copy(out=bias[:], in_=b_cols[:, :M_TILES])
-        res = keep.tile([P, M_TILES, T], F32, name="res", tag="res", align_bytes=256)
-        partial = keep.tile([P, M_TILES, COLS], F32, name="partial", tag="partial")
 
         for m in range(M_TILES):
             open_bank(0, m, 0)
-            open_bank(2, m, 1)
-        for g in range(EARLY):
-            if g > 0 and g % 2 == 0:
-                prepare(load_weights(g, 2))
-            tiles = load_acts(g, 0, 3)
-            prepare([tiles[2], tiles[0], tiles[1]])
+            open_bank(2, m, M_TILES)
+        for g in range(FIRST_GROUP):
+            if g == PASSES_PER_PRODUCT:
+                load_passes(w_stage, weights, g, FIRST_GROUP - g)
+                prepare([w_chunk(i) for i in range(g, FIRST_GROUP)])
+            if g >= PASSES_PER_PRODUCT:
+                load_passes(x_stage, acts, g, 1)
+            elif g % 2 == 0:
+                load_passes(x_stage, acts, g, 2)
+            prepare([x_chunk(g, 2), x_chunk(g, 0), x_chunk(g, 1)])
             multiply_all(g, 2)
             multiply_all(g, 0)
 
         for m in range(M_TILES):
-            drain_partial(m)
-            open_bank(1, m, 1)
-            for g in range(EARLY):
+            drain_with_bias(2, m)
+            open_bank(1, m, M_TILES)
+            for g in range(FIRST_GROUP):
                 multiply(g, 1, m)
 
-        tiles = load_acts(6, 0, 3)
-        prepare(tiles[:2] + load_weights(6, 1) + tiles[2:])
-        multiply_all(6, 0)
-        multiply_all(6, 1)
+        g = LAST - 1
+        load_passes(x_stage, acts, g, 1)
+        load_passes(w_stage, weights, g, 1)
+        prepare([x_chunk(g, 0), x_chunk(g, 1), w_chunk(g), x_chunk(g, 2)])
+        multiply_all(g, 0)
+        multiply_all(g, 1)
 
-        for t in range(3):
-            new_codes(("x", 7, t), E4M3)
-        raw = load_last(0, 640)
-        spans = []
-        for i in range(5):
-            spans.append(copy_span(nc.vector.tensor_copy if i % 2 == 0 else nc.scalar.copy, raw[:, :, i * P : (i + 1) * P]))
-        for i in range(len(spans)):
-            quantise_span(("x", 7, i * P // COLS), i * P % COLS, spans[i])
+        for t in range(T_TILES):
+            new_codes(("x", LAST, t))
+        new_codes(("w", LAST))
+        prepare_piece(0, both[::-1])
+        load_passes(w_stage, weights, LAST, 1)
+        prepare_spans(w_chunk(LAST)[1], 0, lambda t: ("w", LAST), both)
+        multiply_all(LAST, 0)
+        for m in range(M_TILES):
+            drain_with_bias(0, m)
 
-        rows = load_weights(7, 1)[0][1]
-        new_codes(("w", 7), E5M2)
-        spans = []
+        prepare_piece(1, vector_alone)
         for m in range(M_TILES):
-            spans.append(copy_span(nc.vector.tensor_copy if m % 2 == 0 else nc.scalar.copy, rows[:, :, m * P : (m + 1) * P]))
-        for m in range(M_TILES):
-            quantise_span(("w", 7), m * P, spans[m])
-        multiply_all(7, 0)
-        for m in range(M_TILES):
-            drain_on_scalar(0, m)
-
-        raw = load_last(640, 1024)
-        spans = [copy_span(nc.vector.tensor_copy, raw[:, :, i * P : (i + 1) * P]) for i in range(3)]
-        for i in range(len(spans)):
-            quantise_span(("x", 7, (640 + i * P) // COLS), (640 + i * P) % COLS, spans[i])
-
-        for m in range(M_TILES):
-            if m == 2:
-                multiply_all(7, 1)
+            if m == M_TILES // 2:
+                multiply_all(LAST, 1)
             open_bank(2, m, 0)
-            for g in range(EARLY, PASSES - 1):
-                multiply(g, 2, m)
+            multiply(LAST - 1, 2, m)
         for m in range(M_TILES):
-            drain_on_scalar(1, m)
+            drain_with_bias(1, m)
 
-        raw = load_last(1024, 1280)
-        spans = [copy_span(nc.vector.tensor_copy, raw[:, :, i * P : (i + 1) * P]) for i in range(2)]
-        for i in range(len(spans)):
-            quantise_span(("x", 7, (1024 + i * P) // COLS), (1024 + i * P) % COLS, spans[i])
-
-        raw = load_last(1280, 1536)
-        spans = [copy_span(nc.vector.tensor_copy, raw[:, :, i * P : (i + 1) * P]) for i in range(2)]
-        for i in range(len(spans)):
-            quantise_span(("x", 7, (1280 + i * P) // COLS), (1280 + i * P) % COLS, spans[i])
-
-        multiply_all(7, 2)
+        prepare_piece(2, vector_alone)
+        prepare_piece(3, vector_alone)
+        multiply_all(LAST, 2)
         for m in range(M_TILES):
-            drain_onto_partial(m)
+            drain_onto_first_group(m)
 
         for t in range(3):
             for m in range(M_TILES):
-                store(t, t + 1, m, m + 1)
+                store(t, m, m + 1)

@@ -28,8 +28,7 @@ SLOTS = 4
 MX_ALIGN = 64
 DMA_ALIGN = 256
 
-FIRST_GROUP = 6
-PIECES = (0, 640, 1024, 1280, 1536)
+WHOLE = 5
 
 
 def tile_mix_jvp_fm_bias_kernel(tc, w, xd, wd, x, b, out):
@@ -40,7 +39,7 @@ def tile_mix_jvp_fm_bias_kernel(tc, w, xd, wd, x, b, out):
     with ExitStack() as ctx:
         stage = ctx.enter_context(tc.tile_pool(name="stage", bufs=1))
         chunk_pool = ctx.enter_context(tc.tile_pool(name="chunks", bufs=4))
-        span_pool = ctx.enter_context(tc.tile_pool(name="spans", bufs=PIECES[1] // P))
+        span_pool = ctx.enter_context(tc.tile_pool(name="spans", bufs=COLS // P + 1))
         ring = ctx.enter_context(tc.tile_pool(name="ring", bufs=4))
         keep = ctx.enter_context(tc.tile_pool(name="keep", bufs=1))
         psum = ctx.enter_context(tc.psum_pool(name="psum", bufs=1))
@@ -61,10 +60,11 @@ def tile_mix_jvp_fm_bias_kernel(tc, w, xd, wd, x, b, out):
                 in_=src[k0 : k0 + count * K_PASS, :].rearrange("(g p j) c -> p g (j c)", g=count, j=PACK),
             )
 
-        def load_piece(i):
-            c0, c1 = PIECES[i], PIECES[i + 1]
-            rows = x_stage[:, (LAST + i) % SLOTS, : PACK * (c1 - c0)].rearrange("p (j c) -> p j c", j=PACK)
-            nc.sync.dma_start(out=rows, in_=x[K - K_PASS :, c0:c1].rearrange("(p j) c -> p j c", j=PACK))
+        def load_columns(g, c0, c1):
+            k0 = (g % PASSES_PER_PRODUCT) * K_PASS
+            start = PACK * c0
+            rows = x_stage[:, g % SLOTS, start : start + PACK * (c1 - c0)].rearrange("p (j c) -> p j c", j=PACK)
+            nc.sync.dma_start(out=rows, in_=x[k0 : k0 + K_PASS, c0:c1].rearrange("(p j) c -> p j c", j=PACK))
             return rows
 
         def w_chunk(g):
@@ -77,8 +77,7 @@ def tile_mix_jvp_fm_bias_kernel(tc, w, xd, wd, x, b, out):
         def new_codes(key):
             g = key[1]
             fmt = (weights if key[0] == "w" else acts)[g // PASSES_PER_PRODUCT][1]
-            waiting_tile = 1 if g < FIRST_GROUP else 2
-            if key[0] == "x" and g < LAST and key[2] != waiting_tile:
+            if key[0] == "x" and key[2] < 2:
                 pool, label = ring, "ring"
             else:
                 pool, label = keep, "%s%d_%d" % (key[0], g, key[-1])
@@ -130,8 +129,8 @@ def tile_mix_jvp_fm_bias_kernel(tc, w, xd, wd, x, b, out):
                     quantise_span(i - 1)
             quantise_span(len(spans) - 1)
 
-        def prepare_piece(i, copies):
-            prepare_spans(load_piece(i), PIECES[i], lambda t: ("x", LAST, t), copies)
+        def prepare_columns(g, c0, c1, copies):
+            prepare_spans(load_columns(g, c0, c1), c0, lambda t: ("x", g, t), copies)
 
         def open_bank(t, m, first_bank):
             bank = "bank%d" % (first_bank + m)
@@ -147,15 +146,15 @@ def tile_mix_jvp_fm_bias_kernel(tc, w, xd, wd, x, b, out):
                 lhsT_scale=w_scales[:, cols],
                 rhs=x_codes[:].bitcast(x_fmt),
                 rhs_scale=x_scales[:],
-                start=(g == 0 or (t == 2 and g == FIRST_GROUP)),
-                stop=(g == LAST or (t == 2 and g == FIRST_GROUP - 1)),
+                start=(g == 0),
+                stop=(g == LAST),
             )
 
         def multiply_all(g, t):
             for m in range(M_TILES):
                 multiply(g, t, m)
 
-        def drain_with_bias(t, m):
+        def drain_on_scalar(t, m):
             nc.scalar.activation(
                 out=res[:, m, t * COLS : (t + 1) * COLS],
                 in_=acc[t, m][:],
@@ -163,18 +162,24 @@ def tile_mix_jvp_fm_bias_kernel(tc, w, xd, wd, x, b, out):
                 bias=bias[:, m : m + 1],
             )
 
-        def drain_onto_first_group(m):
-            cols = res[:, m, 2 * COLS :]
-            nc.vector.tensor_tensor(out=cols, in0=acc[2, m][:], in1=cols, op=mybir.AluOpType.add)
+        def drain_on_vector(t, m):
+            nc.vector.tensor_scalar(
+                out=res[:, m, t * COLS : (t + 1) * COLS],
+                in0=acc[t, m][:],
+                scalar1=bias[:, m : m + 1],
+                scalar2=None,
+                op0=mybir.AluOpType.add,
+            )
 
-        def store(t, m0, m1):
+        def store(t0, t1, m0, m1):
             nc.sync.dma_start(
-                out=out[m0 * P : m1 * P, t * COLS : (t + 1) * COLS].rearrange("(m p) c -> p m c", p=P),
-                in_=res[:, m0:m1, t * COLS : (t + 1) * COLS],
+                out=out[m0 * P : m1 * P, t0 * COLS : t1 * COLS].rearrange("(m p) c -> p m c", p=P),
+                in_=res[:, m0:m1, t0 * COLS : t1 * COLS],
             )
 
         both = [nc.vector.tensor_copy, nc.scalar.copy]
         vector_alone = [nc.vector.tensor_copy]
+        scalar_alone = [nc.scalar.copy]
 
         load_passes(w_stage, weights, 0, PASSES_PER_PRODUCT)
 
@@ -191,57 +196,60 @@ def tile_mix_jvp_fm_bias_kernel(tc, w, xd, wd, x, b, out):
 
         for m in range(M_TILES):
             open_bank(0, m, 0)
-            open_bank(2, m, M_TILES)
-        for g in range(FIRST_GROUP):
+            open_bank(1, m, M_TILES)
+        for g in range(WHOLE):
             if g == PASSES_PER_PRODUCT:
-                load_passes(w_stage, weights, g, FIRST_GROUP - g)
-                prepare([w_chunk(i) for i in range(g, FIRST_GROUP)])
+                load_passes(w_stage, weights, g, LAST - g)
+                prepare([w_chunk(i) for i in range(g, LAST)])
             if g >= PASSES_PER_PRODUCT:
                 load_passes(x_stage, acts, g, 1)
             elif g % 2 == 0:
                 load_passes(x_stage, acts, g, 2)
-            prepare([x_chunk(g, 2), x_chunk(g, 0), x_chunk(g, 1)])
-            multiply_all(g, 2)
+            prepare([x_chunk(g, t) for t in range(T_TILES)])
             multiply_all(g, 0)
+            multiply_all(g, 1)
+        for g in range(WHOLE, LAST):
+            rows = load_columns(g, 0, 2 * COLS)
+            prepare([(("x", g, 0), rows[:, :, :COLS]), (("x", g, 1), rows[:, :, COLS:])])
+            multiply_all(g, 0)
+            multiply_all(g, 1)
 
-        for m in range(M_TILES):
-            drain_with_bias(2, m)
-            open_bank(1, m, M_TILES)
-            for g in range(FIRST_GROUP):
-                multiply(g, 1, m)
-
-        g = LAST - 1
-        load_passes(x_stage, acts, g, 1)
-        load_passes(w_stage, weights, g, 1)
-        prepare([x_chunk(g, 0), x_chunk(g, 1), w_chunk(g), x_chunk(g, 2)])
-        multiply_all(g, 0)
-        multiply_all(g, 1)
-
-        for t in range(T_TILES):
-            new_codes(("x", LAST, t))
-        new_codes(("w", LAST))
-        prepare_piece(0, both[::-1])
+        prepare([(("x", LAST, 0), load_columns(LAST, 0, COLS))])
         load_passes(w_stage, weights, LAST, 1)
+        new_codes(("w", LAST))
         prepare_spans(w_chunk(LAST)[1], 0, lambda t: ("w", LAST), both)
         multiply_all(LAST, 0)
         for m in range(M_TILES):
-            drain_with_bias(0, m)
+            drain_on_scalar(0, m)
 
-        prepare_piece(1, vector_alone)
+        new_codes(("x", LAST, 1))
+        prepare_columns(LAST, COLS, 2 * COLS, vector_alone)
         for m in range(M_TILES):
             if m == M_TILES // 2:
                 multiply_all(LAST, 1)
             open_bank(2, m, 0)
-            multiply(LAST - 1, 2, m)
+            for g in range(WHOLE):
+                multiply(g, 2, m)
         for m in range(M_TILES):
-            drain_with_bias(1, m)
+            drain_on_scalar(1, m)
 
-        prepare_piece(2, vector_alone)
-        prepare_piece(3, vector_alone)
-        multiply_all(LAST, 2)
+        for g in range(WHOLE, LAST):
+            new_codes(("x", g, 2))
+            prepare_columns(g, 2 * COLS, T, vector_alone)
+        new_codes(("x", LAST, 2))
+        prepare_columns(LAST, 2 * COLS, T - HALF, scalar_alone)
+        prepare_columns(LAST, T - HALF, T, both)
+        for m in range(M_TILES - 1):
+            for g in range(WHOLE, LAST):
+                multiply(g, 2, m)
+        for m in range(M_TILES - 1):
+            multiply(LAST, 2, m)
+        for g in range(WHOLE, PASSES):
+            multiply(g, 2, M_TILES - 1)
         for m in range(M_TILES):
-            drain_onto_first_group(m)
+            (drain_on_scalar if m % 2 == 0 else drain_on_vector)(2, m)
 
-        for t in range(3):
-            for m in range(M_TILES):
-                store(t, m, m + 1)
+        store(0, 2, 0, M_TILES // 2)
+        store(0, 2, M_TILES // 2, M_TILES)
+        for m in range(M_TILES):
+            store(2, 3, m, m + 1)

@@ -179,7 +179,8 @@ def tile_mix_jvp_fm_bias_kernel(tc, w, xd, wd, x, b, out):
 
         both = [nc.vector.tensor_copy, nc.scalar.copy]
         vector_alone = [nc.vector.tensor_copy]
-        scalar_alone = [nc.scalar.copy]
+        scalar_first = [nc.scalar.copy, nc.vector.tensor_copy]
+        scalar_last = vector_alone * (COLS // P - 1) + [nc.scalar.copy]
 
         load_passes(w_stage, weights, 0, PASSES_PER_PRODUCT)
 
@@ -233,12 +234,13 @@ def tile_mix_jvp_fm_bias_kernel(tc, w, xd, wd, x, b, out):
         for m in range(M_TILES):
             drain_on_scalar(1, m)
 
-        for g in range(WHOLE, LAST):
+        for g in range(WHOLE, PASSES):
             new_codes(("x", g, 2))
+        for g in range(WHOLE, LAST - 1):
             prepare_columns(g, 2 * COLS, T, vector_alone)
-        new_codes(("x", LAST, 2))
-        prepare_columns(LAST, 2 * COLS, T - HALF, scalar_alone)
-        prepare_columns(LAST, T - HALF, T, both)
+        prepare_columns(LAST - 1, 2 * COLS, T, scalar_last)
+        prepare_columns(LAST, 2 * COLS, T - HALF, scalar_first)
+        prepare_columns(LAST, T - HALF, T, scalar_first)
         for m in range(M_TILES - 1):
             for g in range(WHOLE, LAST):
                 multiply(g, 2, m)
@@ -251,5 +253,6 @@ def tile_mix_jvp_fm_bias_kernel(tc, w, xd, wd, x, b, out):
 
         store(0, 2, 0, M_TILES // 2)
         store(0, 2, M_TILES // 2, M_TILES)
-        for m in range(M_TILES):
-            store(2, 3, m, m + 1)
+        store(2, T_TILES, 0, 1)
+        store(2, T_TILES, 1, M_TILES - 1)
+        store(2, T_TILES, M_TILES - 1, M_TILES)

@@ -29,6 +29,8 @@ MX_ALIGN = 64
 DMA_ALIGN = 256
 
 WHOLE = 5
+PARTIAL = (1, 3)
+SCALAR_SHARE = {COLS: 160, HALF: 96}
 
 
 def tile_mix_jvp_fm_bias_kernel(tc, w, xd, wd, x, b, out):
@@ -39,7 +41,6 @@ def tile_mix_jvp_fm_bias_kernel(tc, w, xd, wd, x, b, out):
     with ExitStack() as ctx:
         stage = ctx.enter_context(tc.tile_pool(name="stage", bufs=1))
         chunk_pool = ctx.enter_context(tc.tile_pool(name="chunks", bufs=4))
-        span_pool = ctx.enter_context(tc.tile_pool(name="spans", bufs=COLS // P + 1))
         ring = ctx.enter_context(tc.tile_pool(name="ring", bufs=4))
         keep = ctx.enter_context(tc.tile_pool(name="keep", bufs=1))
         psum = ctx.enter_context(tc.psum_pool(name="psum", bufs=1))
@@ -74,10 +75,13 @@ def tile_mix_jvp_fm_bias_kernel(tc, w, xd, wd, x, b, out):
             rows = x_stage[:, g % SLOTS, :].rearrange("p (j c) -> p j c", j=PACK)
             return ("x", g, t), rows[:, :, t * COLS : (t + 1) * COLS]
 
+        def kept(g, t):
+            return t == 2 or (t == 1 and g < PASSES_PER_PRODUCT)
+
         def new_codes(key):
             g = key[1]
             fmt = (weights if key[0] == "w" else acts)[g // PASSES_PER_PRODUCT][1]
-            if key[0] == "x" and key[2] < 2:
+            if key[0] == "x" and not kept(key[1], key[2]):
                 pool, label = ring, "ring"
             else:
                 pool, label = keep, "%s%d_%d" % (key[0], g, key[-1])
@@ -114,24 +118,6 @@ def tile_mix_jvp_fm_bias_kernel(tc, w, xd, wd, x, b, out):
             quantise(waiting[0], HALF, waiting[1][:, HALF:, :])
             quantise(waiting[0], 0, waiting[1][:, :HALF, :])
 
-        def prepare_spans(rows, c0, key_of_tile, copies):
-            spans = []
-
-            def quantise_span(i):
-                t, c = divmod(c0 + i * P, COLS)
-                quantise(key_of_tile(t), c, spans[i][:])
-
-            for i in range(rows.shape[2] // P):
-                span = span_pool.tile([P, P, PACK], BF16, name="span", tag="span", align_bytes=MX_ALIGN)
-                round_and_interleave(copies[i % len(copies)], span[:], rows[:, :, i * P : (i + 1) * P])
-                spans.append(span)
-                if i > 0:
-                    quantise_span(i - 1)
-            quantise_span(len(spans) - 1)
-
-        def prepare_columns(g, c0, c1, copies):
-            prepare_spans(load_columns(g, c0, c1), c0, lambda t: ("x", g, t), copies)
-
         def open_bank(t, m, first_bank):
             bank = "bank%d" % (first_bank + m)
             acc[t, m] = psum.tile([P, COLS], F32, name=bank, tag=bank)
@@ -146,8 +132,8 @@ def tile_mix_jvp_fm_bias_kernel(tc, w, xd, wd, x, b, out):
                 lhsT_scale=w_scales[:, cols],
                 rhs=x_codes[:].bitcast(x_fmt),
                 rhs_scale=x_scales[:],
-                start=(g == 0),
-                stop=(g == LAST),
+                start=(g == 0 or (t == 2 and m in PARTIAL and g == PASSES_PER_PRODUCT)),
+                stop=(g == LAST or (t == 2 and m in PARTIAL and g == PASSES_PER_PRODUCT - 1)),
             )
 
         def multiply_all(g, t):
@@ -171,16 +157,30 @@ def tile_mix_jvp_fm_bias_kernel(tc, w, xd, wd, x, b, out):
                 op0=mybir.AluOpType.add,
             )
 
+        def add_on_vector(t, m):
+            part = res[:, m, t * COLS : (t + 1) * COLS]
+            nc.vector.tensor_tensor(out=part, in0=acc[t, m][:], in1=part, op=mybir.AluOpType.add)
+
+        def prepare_alone(g, c0, width, shared):
+            rows = load_columns(g, c0, c0 + width)
+            t, first = divmod(c0, COLS)
+            half = width // 2
+            own = width - SCALAR_SHARE[width] if shared else width
+            rounded = chunk_pool.tile([P, COLS, PACK], BF16, name="chunk", tag="chunk", align_bytes=MX_ALIGN)
+            if shared:
+                round_and_interleave(nc.scalar.copy, rounded[:, own:width, :], rows[:, :, own:])
+            round_and_interleave(nc.vector.tensor_copy, rounded[:, :half, :], rows[:, :, :half])
+            round_and_interleave(nc.vector.tensor_copy, rounded[:, half:own, :], rows[:, :, half:own])
+            if first == 0:
+                new_codes(("x", g, t))
+            quantise(("x", g, t), first, rounded[:, :half, :])
+            quantise(("x", g, t), first + half, rounded[:, half:width, :])
+
         def store(t0, t1, m0, m1):
             nc.sync.dma_start(
                 out=out[m0 * P : m1 * P, t0 * COLS : t1 * COLS].rearrange("(m p) c -> p m c", p=P),
                 in_=res[:, m0:m1, t0 * COLS : t1 * COLS],
             )
-
-        both = [nc.vector.tensor_copy, nc.scalar.copy]
-        vector_alone = [nc.vector.tensor_copy]
-        scalar_first = [nc.scalar.copy, nc.vector.tensor_copy]
-        scalar_last = vector_alone * (COLS // P - 1) + [nc.scalar.copy]
 
         load_passes(w_stage, weights, 0, PASSES_PER_PRODUCT)
 
@@ -193,14 +193,14 @@ def tile_mix_jvp_fm_bias_kernel(tc, w, xd, wd, x, b, out):
         prepare([w_chunk(g) for g in range(PASSES_PER_PRODUCT)])
         b_cols = psum.tile([P, P], F32, name="b_cols", tag="bank%d" % (2 * M_TILES - 1))
         nc.tensor.transpose(b_cols[:], b_rows[:], ident[:])
-        nc.scalar.copy(out=bias[:], in_=b_cols[:, :M_TILES])
+        nc.scalar.activation(out=bias[:], in_=b_cols[:, :M_TILES], func=mybir.ActivationFunctionType.Identity)
 
         for m in range(M_TILES):
             open_bank(0, m, 0)
-            open_bank(1, m, M_TILES)
+            open_bank(2 if m in PARTIAL else 1, m, M_TILES)
         for g in range(WHOLE):
             if g == PASSES_PER_PRODUCT:
-                load_passes(w_stage, weights, g, LAST - g)
+                load_passes(w_stage, weights, PASSES_PER_PRODUCT, LAST - g)
                 prepare([w_chunk(i) for i in range(g, LAST)])
             if g >= PASSES_PER_PRODUCT:
                 load_passes(x_stage, acts, g, 1)
@@ -208,7 +208,14 @@ def tile_mix_jvp_fm_bias_kernel(tc, w, xd, wd, x, b, out):
                 load_passes(x_stage, acts, g, 2)
             prepare([x_chunk(g, t) for t in range(T_TILES)])
             multiply_all(g, 0)
-            multiply_all(g, 1)
+            for m in range(M_TILES):
+                multiply(g, 2 if m in PARTIAL and g < PASSES_PER_PRODUCT else 1, m)
+            if g == PASSES_PER_PRODUCT - 1:
+                for m in PARTIAL:
+                    drain_on_scalar(2, m)
+                    open_bank(1, m, M_TILES)
+                    for i in range(PASSES_PER_PRODUCT):
+                        multiply(i, 1, m)
         for g in range(WHOLE, LAST):
             rows = load_columns(g, 0, 2 * COLS)
             prepare([(("x", g, 0), rows[:, :, :COLS]), (("x", g, 1), rows[:, :, COLS:])])
@@ -218,38 +225,49 @@ def tile_mix_jvp_fm_bias_kernel(tc, w, xd, wd, x, b, out):
         prepare([(("x", LAST, 0), load_columns(LAST, 0, COLS))])
         load_passes(w_stage, weights, LAST, 1)
         new_codes(("w", LAST))
-        prepare_spans(w_chunk(LAST)[1], 0, lambda t: ("w", LAST), both)
-        multiply_all(LAST, 0)
-        for m in range(M_TILES):
-            drain_on_scalar(0, m)
+        last_w = w_chunk(LAST)[1]
 
-        new_codes(("x", LAST, 1))
-        prepare_columns(LAST, COLS, 2 * COLS, vector_alone)
-        for m in range(M_TILES):
-            if m == M_TILES // 2:
-                multiply_all(LAST, 1)
+        def catch_up(m):
             open_bank(2, m, 0)
-            for g in range(WHOLE):
+            for g in range(PASSES_PER_PRODUCT if m in PARTIAL else 0, WHOLE):
                 multiply(g, 2, m)
+
+        rounded = chunk_pool.tile([P, COLS, PACK], BF16, name="chunk", tag="chunk", align_bytes=MX_ALIGN)
+
+        def round_span(copy, m):
+            round_and_interleave(copy, rounded[:, m * P : (m + 1) * P, :], last_w[:, :, m * P : (m + 1) * P])
+
+        def close_tile_0(m):
+            quantise(("w", LAST), m * P, rounded[:, m * P : (m + 1) * P, :])
+            multiply(LAST, 0, m)
+
+        round_span(nc.scalar.copy, 2)
+        round_span(nc.vector.tensor_copy, 0)
+        round_span(nc.vector.tensor_copy, 1)
+        close_tile_0(0)
+        round_span(nc.vector.tensor_copy, 3)
+        for m in range(1, M_TILES):
+            close_tile_0(m)
+
+        drain_on_scalar(0, 0)
+        prepare_alone(LAST, COLS, COLS, True)
+        drain_on_scalar(0, 1)
+        drain_on_scalar(0, 2)
+        drain_on_vector(0, 3)
+        catch_up(0)
+        multiply_all(LAST, 1)
+        for m in range(1, M_TILES):
+            catch_up(m)
         for m in range(M_TILES):
             drain_on_scalar(1, m)
-
-        for g in range(WHOLE, PASSES):
-            new_codes(("x", g, 2))
-        for g in range(WHOLE, LAST - 1):
-            prepare_columns(g, 2 * COLS, T, vector_alone)
-        prepare_columns(LAST - 1, 2 * COLS, T, scalar_last)
-        prepare_columns(LAST, 2 * COLS, T - HALF, scalar_first)
-        prepare_columns(LAST, T - HALF, T, scalar_first)
-        for m in range(M_TILES - 1):
-            for g in range(WHOLE, LAST):
-                multiply(g, 2, m)
-        for m in range(M_TILES - 1):
-            multiply(LAST, 2, m)
-        for g in range(WHOLE, PASSES):
-            multiply(g, 2, M_TILES - 1)
+        for g in range(WHOLE, LAST):
+            prepare_alone(g, 2 * COLS, COLS, g == LAST - 1)
+            multiply_all(g, 2)
+        prepare_alone(LAST, 2 * COLS, HALF, True)
+        prepare_alone(LAST, T - HALF, HALF, True)
+        multiply_all(LAST, 2)
         for m in range(M_TILES):
-            (drain_on_scalar if m % 2 == 0 else drain_on_vector)(2, m)
+            (add_on_vector if m in PARTIAL else drain_on_scalar)(2, m)
 
         store(0, 2, 0, M_TILES // 2)
         store(0, 2, M_TILES // 2, M_TILES)

@@ -260,10 +260,26 @@ def tile_mix_jvp_fm_bias_kernel(tc, w, xd, wd, x, b, out):
             catch_up(m)
         for m in range(M_TILES):
             drain_on_scalar(1, m)
-        for g in range(WHOLE, LAST):
-            prepare_alone(g, 2 * COLS, COLS, g == LAST - 1)
-            multiply_all(g, 2)
-        prepare_alone(LAST, 2 * COLS, HALF, True)
+        prepare_alone(WHOLE, 2 * COLS, COLS, False)
+        multiply_all(WHOLE, 2)
+        g = LAST - 1
+        rows = load_columns(g, 2 * COLS, T)
+        first_half = load_columns(LAST, 2 * COLS, T - HALF)
+        rounded = chunk_pool.tile([P, COLS, PACK], BF16, name="chunk", tag="chunk", align_bytes=MX_ALIGN)
+        rounded_half = chunk_pool.tile([P, COLS, PACK], BF16, name="chunk", tag="chunk", align_bytes=MX_ALIGN)
+        own = COLS - SCALAR_SHARE[COLS]
+        round_and_interleave(nc.scalar.copy, rounded[:, own:, :], rows[:, :, own:])
+        round_and_interleave(nc.scalar.copy, rounded_half[:, P:HALF, :], first_half[:, :, P:])
+        round_and_interleave(nc.vector.tensor_copy, rounded[:, :HALF, :], rows[:, :, :HALF])
+        round_and_interleave(nc.vector.tensor_copy, rounded[:, HALF:own, :], rows[:, :, HALF:own])
+        new_codes(("x", g, 2))
+        new_codes(("x", LAST, 2))
+        quantise(("x", g, 2), 0, rounded[:, :HALF, :])
+        round_and_interleave(nc.vector.tensor_copy, rounded_half[:, :P, :], first_half[:, :, :P])
+        quantise(("x", g, 2), HALF, rounded[:, HALF:, :])
+        multiply_all(g, 2)
+        quantise(("x", LAST, 2), 0, rounded_half[:, :P, :])
+        quantise(("x", LAST, 2), P, rounded_half[:, P:HALF, :])
         prepare_alone(LAST, T - HALF, HALF, True)
         multiply_all(LAST, 2)
         for m in range(M_TILES):

@@ -28,6 +28,8 @@ SLOTS = 4
 MX_ALIGN = 64
 DMA_ALIGN = 256
 
+AHEAD = 7
+W_SECOND = 3
 WHOLE = 5
 PARTIAL = (1, 3)
 SCALAR_SHARE = {COLS: 160, HALF: 96}
@@ -182,7 +184,7 @@ def tile_mix_jvp_fm_bias_kernel(tc, w, xd, wd, x, b, out):
                 in_=res[:, m0:m1, t0 * COLS : t1 * COLS],
             )
 
-        load_passes(w_stage, weights, 0, PASSES_PER_PRODUCT)
+        load_passes(x_stage, acts, 0, PASSES_PER_PRODUCT)
 
         b_rows = keep.tile([P, P], F32, name="b_rows", tag="b_rows")
         ident = keep.tile([P, P], F32, name="ident", tag="ident")
@@ -190,32 +192,34 @@ def tile_mix_jvp_fm_bias_kernel(tc, w, xd, wd, x, b, out):
         nc.vector.memset(b_rows[:], 0.0)
         nc.sync.dma_start(out=b_rows[:M_TILES, :], in_=b.rearrange("(m p) -> m p", p=P))
         make_identity(nc, ident[:])
-        prepare([w_chunk(g) for g in range(PASSES_PER_PRODUCT)])
+        load_passes(w_stage, weights, 0, PASSES_PER_PRODUCT)
         b_cols = psum.tile([P, P], F32, name="b_cols", tag="bank%d" % (2 * M_TILES - 1))
         nc.tensor.transpose(b_cols[:], b_rows[:], ident[:])
         nc.scalar.activation(out=bias[:], in_=b_cols[:, :M_TILES], func=mybir.ActivationFunctionType.Identity)
 
+        xd_chunks = [x_chunk(g, t) for g in range(PASSES_PER_PRODUCT) for t in range(T_TILES)]
+        prepare(xd_chunks[:AHEAD])
+        load_passes(x_stage, acts, PASSES_PER_PRODUCT, 1)
+        prepare([w_chunk(g) for g in range(PASSES_PER_PRODUCT)])
+        load_passes(w_stage, weights, PASSES_PER_PRODUCT, W_SECOND)
+        prepare(xd_chunks[AHEAD:])
         for m in range(M_TILES):
             open_bank(0, m, 0)
             open_bank(2 if m in PARTIAL else 1, m, M_TILES)
-        for g in range(WHOLE):
-            if g == PASSES_PER_PRODUCT:
-                load_passes(w_stage, weights, PASSES_PER_PRODUCT, LAST - g)
-                prepare([w_chunk(i) for i in range(g, LAST)])
-            if g >= PASSES_PER_PRODUCT:
-                load_passes(x_stage, acts, g, 1)
-            elif g % 2 == 0:
-                load_passes(x_stage, acts, g, 2)
-            prepare([x_chunk(g, t) for t in range(T_TILES)])
-            multiply_all(g, 0)
+        for g in range(PASSES_PER_PRODUCT):
             for m in range(M_TILES):
-                multiply(g, 2 if m in PARTIAL and g < PASSES_PER_PRODUCT else 1, m)
-            if g == PASSES_PER_PRODUCT - 1:
-                for m in PARTIAL:
-                    drain_on_scalar(2, m)
-                    open_bank(1, m, M_TILES)
-                    for i in range(PASSES_PER_PRODUCT):
-                        multiply(i, 1, m)
+                multiply(g, 2 if m in PARTIAL else 1, m)
+            multiply_all(g, 0)
+        g = PASSES_PER_PRODUCT
+        prepare([x_chunk(g, t) for t in reversed(range(T_TILES))])
+        for m in PARTIAL:
+            drain_on_scalar(2, m)
+            open_bank(1, m, M_TILES)
+            for i in range(PASSES_PER_PRODUCT):
+                multiply(i, 1, m)
+        prepare([w_chunk(i) for i in range(g, g + W_SECOND)])
+        multiply_all(g, 0)
+        multiply_all(g, 1)
         for g in range(WHOLE, LAST):
             rows = load_columns(g, 0, 2 * COLS)
             prepare([(("x", g, 0), rows[:, :, :COLS]), (("x", g, 1), rows[:, :, COLS:])])

@@ -12,285 +12,312 @@ U32 = mybir.dt.uint32
 U8 = mybir.dt.uint8
 E4M3 = mybir.dt.float8_e4m3fn_x4
 E5M2 = mybir.dt.float8_e5m2_x4
+ADD = mybir.AluOpType.add
+IDENTITY = mybir.ActivationFunctionType.Identity
 
 P = 128
 PACK = 4
 K_PASS = P * PACK
 COLS = 512
 HALF = COLS // 2
-PASSES_PER_PRODUCT = K // K_PASS
-PASSES = 2 * PASSES_PER_PRODUCT
-LAST = PASSES - 1
+PER = K // K_PASS
+LAST = 2 * PER - 1
 M_TILES = M // P
-T_TILES = T // COLS
 RUN = 4
-SLOTS = 4
 MX_ALIGN = 64
 DMA_ALIGN = 256
 
+SPANS = {"A": (0, COLS), "A2": (COLS, HALF), "B0": (3 * HALF, HALF), "B1": (4 * HALF, HALF), "B2": (5 * HALF, HALF)}
+EARLY = COLS + HALF
+X_SLOT = PACK * T
+W_SLOT = PACK * M
+X0 = 0
+W0 = X0 + PER * X_SLOT
+STAGE = W0 + PER * W_SLOT
 AHEAD = 7
-W_SECOND = 3
-WHOLE = 5
-PARTIAL = (1, 3)
-SCALAR_SHARE = {COLS: 160, HALF: 96}
+CUT = COLS
 
 
 def tile_mix_jvp_fm_bias_kernel(tc, w, xd, wd, x, b, out):
     nc = tc.nc
-    weights = [(w, E4M3), (wd, E5M2)]
-    acts = [(xd, E5M2), (x, E4M3)]
 
     with ExitStack() as ctx:
-        stage = ctx.enter_context(tc.tile_pool(name="stage", bufs=1))
+        stage_pool = ctx.enter_context(tc.tile_pool(name="stage", bufs=1))
         chunk_pool = ctx.enter_context(tc.tile_pool(name="chunks", bufs=4))
-        ring = ctx.enter_context(tc.tile_pool(name="ring", bufs=4))
         keep = ctx.enter_context(tc.tile_pool(name="keep", bufs=1))
         psum = ctx.enter_context(tc.psum_pool(name="psum", bufs=1))
         ctx.enter_context(tc.manual_schedule())
 
-        w_stage = stage.tile([P, SLOTS, PACK * M], F32, name="w_stage", tag="w_stage", align_bytes=DMA_ALIGN)
-        x_stage = stage.tile([P, SLOTS, PACK * T], F32, name="x_stage", tag="x_stage", align_bytes=DMA_ALIGN)
-        res = stage.tile([P, M_TILES, T], F32, name="res", tag="res", align_bytes=DMA_ALIGN)
+        stage = stage_pool.tile([P, STAGE], F32, name="stage", tag="stage", align_bytes=DMA_ALIGN)
+        res = stage_pool.tile([P, M_TILES, T], F32, name="res", tag="res", align_bytes=DMA_ALIGN)
 
-        quantised = {}
+        codes_of = {}
         acc = {}
+        fresh = {}
 
-        def load_passes(staging, operands, g, count):
-            src = operands[g // PASSES_PER_PRODUCT][0]
-            k0 = (g % PASSES_PER_PRODUCT) * K_PASS
+        def load_passes(src, first, count, at):
+            width = src.shape[1]
+            rows = stage[:, at : at + count * PACK * width].rearrange("p (g r) -> p g r", g=count)
             nc.sync.dma_start(
-                out=staging[:, g % SLOTS : g % SLOTS + count, :],
-                in_=src[k0 : k0 + count * K_PASS, :].rearrange("(g p j) c -> p g (j c)", g=count, j=PACK),
+                out=rows,
+                in_=src[first * K_PASS : (first + count) * K_PASS, :].rearrange("(g p j) c -> p g (j c)", g=count, j=PACK),
             )
+            return [rows[:, g, :].rearrange("p (j c) -> p j c", j=PACK) for g in range(count)]
 
-        def load_columns(g, c0, c1):
-            k0 = (g % PASSES_PER_PRODUCT) * K_PASS
-            start = PACK * c0
-            rows = x_stage[:, g % SLOTS, start : start + PACK * (c1 - c0)].rearrange("p (j c) -> p j c", j=PACK)
+        def load_columns(g, c0, c1, at):
+            k0 = (g - PER) * K_PASS
+            rows = stage[:, at : at + PACK * (c1 - c0)].rearrange("p (j c) -> p j c", j=PACK)
             nc.sync.dma_start(out=rows, in_=x[k0 : k0 + K_PASS, c0:c1].rearrange("(p j) c -> p j c", j=PACK))
             return rows
 
-        def w_chunk(g):
-            return ("w", g), w_stage[:, g % SLOTS, :].rearrange("p (j c) -> p j c", j=PACK)
+        def new_codes(key, width, label):
+            codes = keep.tile([P, width], U32, name="codes_" + label, tag="codes_" + label, align_bytes=MX_ALIGN)
+            scales = keep.tile([P, width], U8, name="scales_" + label, tag="scales_" + label, align_bytes=MX_ALIGN)
+            codes_of[key] = (codes, scales)
 
-        def x_chunk(g, t):
-            rows = x_stage[:, g % SLOTS, :].rearrange("p (j c) -> p j c", j=PACK)
-            return ("x", g, t), rows[:, :, t * COLS : (t + 1) * COLS]
-
-        def kept(g, t):
-            return t == 2 or (t == 1 and g < PASSES_PER_PRODUCT)
-
-        def new_codes(key):
-            g = key[1]
-            fmt = (weights if key[0] == "w" else acts)[g // PASSES_PER_PRODUCT][1]
-            if key[0] == "x" and not kept(key[1], key[2]):
-                pool, label = ring, "ring"
+        def operand(kind, g, c0, width):
+            if kind == "w":
+                key, fmt = ("w", g), (E4M3 if g < PER else E5M2)
+                if key not in codes_of:
+                    new_codes(key, M, "w%d" % g)
             else:
-                pool, label = keep, "%s%d_%d" % (key[0], g, key[-1])
-            codes = pool.tile([P, COLS], U32, name="codes_" + label, tag="codes_" + label, align_bytes=MX_ALIGN)
-            scales = pool.tile([P, COLS], U8, name="scales_" + label, tag="scales_" + label, align_bytes=MX_ALIGN)
-            quantised[key] = (codes, scales, fmt)
+                fmt = E5M2 if g < PER else E4M3
+                if c0 < COLS:
+                    key = ("first", g)
+                    if key not in codes_of:
+                        new_codes(key, COLS, "first%d" % (g if g <= PER + 1 else g - PER))
+                elif c0 >= T - HALF:
+                    key = ("end", g)
+                    c0 = c0 - (T - HALF)
+                    if key not in codes_of:
+                        new_codes(key, HALF, "end%d" % g)
+                else:
+                    key = ("rest", g)
+                    c0 = c0 - COLS
+                    if key not in codes_of:
+                        new_codes(key, T - COLS - HALF, "rest%d" % (g % PER))
+            codes, scales = codes_of[key]
+            return codes[:, c0 : c0 + width].bitcast(fmt), scales[:, c0 : c0 + width]
 
-        def round_and_interleave(copy, rounded, rows):
+        def new_chunk():
+            return chunk_pool.tile([P, COLS, PACK], BF16, name="chunk", tag="chunk", align_bytes=MX_ALIGN)
+
+        def round_on(copy, rounded, rows, c0, c1):
             copy(
-                out=rounded.rearrange("p (c i) j -> p c j i", i=RUN),
-                in_=rows.rearrange("p j (c i) -> p c j i", i=RUN),
+                out=rounded[:, c0:c1, :].rearrange("p (c i) j -> p c j i", i=RUN),
+                in_=rows[:, :, c0:c1].rearrange("p j (c i) -> p c j i", i=RUN),
             )
 
-        def quantise(key, c0, rounded):
-            codes, scales, fmt = quantised[key]
-            c1 = c0 + rounded.shape[1]
-            nc.vector.quantize_mx(
-                out=codes[:, c0:c1].bitcast(fmt),
-                scales=scales[:, c0:c1],
-                in_=rounded.rearrange("p c j -> p (c j)"),
-            )
+        def quantise(kind, g, col, rounded, c0, c1):
+            if kind == "x" and col + c0 < T - HALF < col + c1:
+                quantise(kind, g, col, rounded, c0, T - HALF - col)
+                quantise(kind, g, col, rounded, T - HALF - col, c1)
+                return
+            codes, scales = operand(kind, g, col + c0, c1 - c0)
+            nc.vector.quantize_mx(out=codes, scales=scales, in_=rounded[:, c0:c1, :].rearrange("p c j -> p (c j)"))
 
         def prepare(chunks):
             waiting = None
-            for key, rows in chunks:
-                rounded = chunk_pool.tile([P, COLS, PACK], BF16, name="chunk", tag="chunk", align_bytes=MX_ALIGN)
-                round_and_interleave(nc.scalar.copy, rounded[:, :HALF, :], rows[:, :, :HALF])
-                round_and_interleave(nc.vector.tensor_copy, rounded[:, HALF:, :], rows[:, :, HALF:])
+            for kind, g, col, rows in chunks:
+                width = rows.shape[2]
+                rounded = new_chunk()
+                round_on(nc.scalar.copy, rounded, rows, 0, width // 2)
+                round_on(nc.vector.tensor_copy, rounded, rows, width // 2, width)
                 if waiting is not None:
-                    new_codes(waiting[0])
-                    quantise(waiting[0], 0, waiting[1][:])
-                waiting = (key, rounded)
-            new_codes(waiting[0])
-            quantise(waiting[0], HALF, waiting[1][:, HALF:, :])
-            quantise(waiting[0], 0, waiting[1][:, :HALF, :])
+                    quantise(*waiting[:4], 0, waiting[4])
+                waiting = (kind, g, col, rounded, width)
+            width = waiting[4]
+            quantise(*waiting[:4], width // 2, width)
+            quantise(*waiting[:4], 0, width // 2)
 
-        def open_bank(t, m, first_bank):
-            bank = "bank%d" % (first_bank + m)
-            acc[t, m] = psum.tile([P, COLS], F32, name=bank, tag=bank)
+        def x_chunks(g, rows, col):
+            width = rows.shape[2]
+            return [("x", g, col + c, rows[:, :, c : min(c + COLS, width)]) for c in range(0, width, COLS)]
 
-        def multiply(g, t, m):
-            w_codes, w_scales, w_fmt = quantised["w", g]
-            x_codes, x_scales, x_fmt = quantised["x", g, t]
-            cols = slice(m * P, (m + 1) * P)
-            nc.tensor.matmul_mx(
-                out=acc[t, m][:],
-                lhsT=w_codes[:, cols].bitcast(w_fmt),
-                lhsT_scale=w_scales[:, cols],
-                rhs=x_codes[:].bitcast(x_fmt),
-                rhs_scale=x_scales[:],
-                start=(g == 0 or (t == 2 and m in PARTIAL and g == PASSES_PER_PRODUCT)),
-                stop=(g == LAST or (t == 2 and m in PARTIAL and g == PASSES_PER_PRODUCT - 1)),
-            )
+        def open_bank(span, i, bank):
+            acc[span, i] = psum.tile([P, COLS], F32, name="bank%d" % bank, tag="bank%d" % bank)
+            fresh[span, i] = True
 
-        def multiply_all(g, t):
-            for m in range(M_TILES):
-                multiply(g, t, m)
+        def rows_of(span, i):
+            return [i] if SPANS[span][1] == COLS else [2 * i, 2 * i + 1]
 
-        def drain_on_scalar(t, m):
-            nc.scalar.activation(
-                out=res[:, m, t * COLS : (t + 1) * COLS],
-                in_=acc[t, m][:],
-                func=mybir.ActivationFunctionType.Identity,
-                bias=bias[:, m : m + 1],
-            )
+        def multiply(g, span, i, stop, c0=0, c1=None, only=None):
+            col, width = SPANS[span]
+            c1 = width if c1 is None else c1
+            ms = rows_of(span, i)
+            for n, m in enumerate(ms):
+                if only is not None and m != only:
+                    continue
+                w_codes, w_scales = operand("w", g, m * P, P)
+                x_codes, x_scales = operand("x", g, col + c0, c1 - c0)
+                nc.tensor.matmul_mx(
+                    out=acc[span, i][:, n * width + c0 : n * width + c1],
+                    lhsT=w_codes,
+                    lhsT_scale=w_scales,
+                    rhs=x_codes,
+                    rhs_scale=x_scales,
+                    start=fresh[span, i],
+                    stop=(stop and m == ms[-1]),
+                )
+                fresh[span, i] = False
 
-        def drain_on_vector(t, m):
-            nc.vector.tensor_scalar(
-                out=res[:, m, t * COLS : (t + 1) * COLS],
-                in0=acc[t, m][:],
-                scalar1=bias[:, m : m + 1],
-                scalar2=None,
-                op0=mybir.AluOpType.add,
-            )
+        def drain(on_scalar, span, i):
+            col, width = SPANS[span]
+            for n, m in enumerate(rows_of(span, i)):
+                dst = res[:, m, col : col + width]
+                src = acc[span, i][:, n * width : (n + 1) * width]
+                if on_scalar:
+                    nc.scalar.activation(out=dst, in_=src, func=IDENTITY, bias=bias[:, m : m + 1])
+                else:
+                    nc.vector.tensor_scalar(out=dst, in0=src, scalar1=bias[:, m : m + 1], scalar2=None, op0=ADD)
 
-        def add_on_vector(t, m):
-            part = res[:, m, t * COLS : (t + 1) * COLS]
-            nc.vector.tensor_tensor(out=part, in0=acc[t, m][:], in1=part, op=mybir.AluOpType.add)
+        def add(span, i):
+            col, width = SPANS[span]
+            ms = rows_of(span, i)
+            part = res[:, ms[0] : ms[-1] + 1, col : col + width]
+            src = acc[span, i][:].rearrange("p (n c) -> p n c", c=width)
+            nc.vector.tensor_tensor(out=part, in0=src, in1=part, op=ADD)
 
-        def prepare_alone(g, c0, width, shared):
-            rows = load_columns(g, c0, c0 + width)
-            t, first = divmod(c0, COLS)
-            half = width // 2
-            own = width - SCALAR_SHARE[width] if shared else width
-            rounded = chunk_pool.tile([P, COLS, PACK], BF16, name="chunk", tag="chunk", align_bytes=MX_ALIGN)
-            if shared:
-                round_and_interleave(nc.scalar.copy, rounded[:, own:width, :], rows[:, :, own:])
-            round_and_interleave(nc.vector.tensor_copy, rounded[:, :half, :], rows[:, :, :half])
-            round_and_interleave(nc.vector.tensor_copy, rounded[:, half:own, :], rows[:, :, half:own])
-            if first == 0:
-                new_codes(("x", g, t))
-            quantise(("x", g, t), first, rounded[:, :half, :])
-            quantise(("x", g, t), first + half, rounded[:, half:width, :])
-
-        def store(t0, t1, m0, m1):
+        def store(c0, c1, m0, step):
             nc.sync.dma_start(
-                out=out[m0 * P : m1 * P, t0 * COLS : t1 * COLS].rearrange("(m p) c -> p m c", p=P),
-                in_=res[:, m0:m1, t0 * COLS : t1 * COLS],
+                out=out[:, c0:c1].rearrange("(m p) c -> p m c", p=P)[:, m0::step, :],
+                in_=res[:, m0::step, c0:c1],
             )
 
-        load_passes(x_stage, acts, 0, PASSES_PER_PRODUCT)
-
+        xd_rows = load_passes(xd, 0, PER, X0)
         b_rows = keep.tile([P, P], F32, name="b_rows", tag="b_rows")
         ident = keep.tile([P, P], F32, name="ident", tag="ident")
         bias = keep.tile([P, M_TILES], F32, name="bias", tag="bias")
         nc.vector.memset(b_rows[:], 0.0)
         nc.sync.dma_start(out=b_rows[:M_TILES, :], in_=b.rearrange("(m p) -> m p", p=P))
         make_identity(nc, ident[:])
-        load_passes(w_stage, weights, 0, PASSES_PER_PRODUCT)
-        b_cols = psum.tile([P, P], F32, name="b_cols", tag="bank%d" % (2 * M_TILES - 1))
+        w_rows = load_passes(w, 0, PER, W0)
+        b_cols = psum.tile([P, P], F32, name="b_cols", tag="bank7")
         nc.tensor.transpose(b_cols[:], b_rows[:], ident[:])
-        nc.scalar.activation(out=bias[:], in_=b_cols[:, :M_TILES], func=mybir.ActivationFunctionType.Identity)
+        nc.scalar.activation(out=bias[:], in_=b_cols[:, :M_TILES], func=IDENTITY)
 
-        xd_chunks = [x_chunk(g, t) for g in range(PASSES_PER_PRODUCT) for t in range(T_TILES)]
+        xd_chunks = [c for g in range(PER) for c in x_chunks(g, xd_rows[g], 0)]
         prepare(xd_chunks[:AHEAD])
-        load_passes(x_stage, acts, PASSES_PER_PRODUCT, 1)
-        prepare([w_chunk(g) for g in range(PASSES_PER_PRODUCT)])
-        load_passes(w_stage, weights, PASSES_PER_PRODUCT, W_SECOND)
+        wd_rows = load_passes(wd, 0, PER - 1, X0)
+        x4_rows = load_passes(x, 0, 1, X0 + X_SLOT)[0]
+        prepare([("w", g, 0, w_rows[g]) for g in range(PER)])
         prepare(xd_chunks[AHEAD:])
-        for m in range(M_TILES):
-            open_bank(0, m, 0)
-            open_bank(2 if m in PARTIAL else 1, m, M_TILES)
-        for g in range(PASSES_PER_PRODUCT):
-            for m in range(M_TILES):
-                multiply(g, 2 if m in PARTIAL else 1, m)
-            multiply_all(g, 0)
-        g = PASSES_PER_PRODUCT
-        prepare([x_chunk(g, t) for t in reversed(range(T_TILES))])
-        for m in PARTIAL:
-            drain_on_scalar(2, m)
-            open_bank(1, m, M_TILES)
-            for i in range(PASSES_PER_PRODUCT):
-                multiply(i, 1, m)
-        prepare([w_chunk(i) for i in range(g, g + W_SECOND)])
-        multiply_all(g, 0)
-        multiply_all(g, 1)
-        for g in range(WHOLE, LAST):
-            rows = load_columns(g, 0, 2 * COLS)
-            prepare([(("x", g, 0), rows[:, :, :COLS]), (("x", g, 1), rows[:, :, COLS:])])
-            multiply_all(g, 0)
-            multiply_all(g, 1)
+        x5_rows = load_passes(x, 1, 1, X0 + 2 * X_SLOT)[0]
+        x6_early = load_columns(LAST - 1, 0, EARLY, W0)
+        x7_early = load_columns(LAST, 0, EARLY, W0 + PACK * EARLY)
+        w7_rows = load_passes(wd, PER - 1, 1, W0 + 2 * PACK * EARLY)[0]
+        late = X0 + 3 * X_SLOT
+        x6_late = load_columns(LAST - 1, EARLY, T, late)
+        x7_first = load_columns(LAST, EARLY, EARLY + CUT, late + PACK * EARLY)
+        x7_second = load_columns(LAST, EARLY + CUT, T, late + PACK * (EARLY + CUT))
 
-        prepare([(("x", LAST, 0), load_columns(LAST, 0, COLS))])
-        load_passes(w_stage, weights, LAST, 1)
-        new_codes(("w", LAST))
-        last_w = w_chunk(LAST)[1]
+        twice = [("B0", 0), ("B1", 0), ("B2", 0)]
+        stay = [("A", 3), ("A2", 0), ("A2", 1), ("B0", 1), ("B1", 1)]
+        for bank, key in enumerate(twice + stay):
+            open_bank(*key, bank)
+        for g in range(PER):
+            for key in twice + stay:
+                multiply(g, *key, False)
+        prepare([("w", PER + i, 0, wd_rows[i]) for i in range(PER - 1)])
+        prepare(x_chunks(PER, x4_rows, 0)[::-1])
+        for key in reversed(twice):
+            multiply(PER, *key, True)
+        for key in reversed(stay):
+            multiply(PER, *key, False)
+        for bank in reversed(range(len(twice))):
+            drain(True, *twice[bank])
+            open_bank("A", bank, bank)
+            for g in range(PER + 1):
+                multiply(g, "A", bank, False)
+        moved = [("A", m) for m in range(len(twice))]
+        prepare(x_chunks(PER + 1, x5_rows, 0))
+        for key in moved + stay:
+            multiply(PER + 1, *key, False)
+        prepare(x_chunks(LAST - 1, x6_early, 0))
+        for key in moved + stay[:3]:
+            multiply(LAST - 1, *key, False)
+        prepare(x_chunks(LAST, x7_early, 0))
 
-        def catch_up(m):
-            open_bank(2, m, 0)
-            for g in range(PASSES_PER_PRODUCT if m in PARTIAL else 0, WHOLE):
-                multiply(g, 2, m)
+        rounded = new_chunk()
 
-        rounded = chunk_pool.tile([P, COLS, PACK], BF16, name="chunk", tag="chunk", align_bytes=MX_ALIGN)
+        def close_rows(m):
+            quantise("w", LAST, 0, rounded, m * P, (m + 1) * P)
+            multiply(LAST, "A", m, True)
+            multiply(LAST, "A2", m // 2, True, only=m)
 
-        def round_span(copy, m):
-            round_and_interleave(copy, rounded[:, m * P : (m + 1) * P, :], last_w[:, :, m * P : (m + 1) * P])
-
-        def close_tile_0(m):
-            quantise(("w", LAST), m * P, rounded[:, m * P : (m + 1) * P, :])
-            multiply(LAST, 0, m)
-
-        round_span(nc.scalar.copy, 2)
-        round_span(nc.vector.tensor_copy, 0)
-        round_span(nc.vector.tensor_copy, 1)
-        close_tile_0(0)
-        round_span(nc.vector.tensor_copy, 3)
+        round_on(nc.scalar.copy, rounded, w7_rows, 2 * P, 3 * P)
+        round_on(nc.vector.tensor_copy, rounded, w7_rows, 0, P)
+        round_on(nc.vector.tensor_copy, rounded, w7_rows, P, 2 * P)
+        close_rows(0)
+        round_on(nc.vector.tensor_copy, rounded, w7_rows, 3 * P, 4 * P)
         for m in range(1, M_TILES):
-            close_tile_0(m)
+            close_rows(m)
+        drain(True, "A", 0)
+        drain(False, "A", 1)
+        drain(True, "A2", 0)
+        drain(False, "A", 2)
+        drain(True, "A", 3)
 
-        drain_on_scalar(0, 0)
-        prepare_alone(LAST, COLS, COLS, True)
-        drain_on_scalar(0, 1)
-        drain_on_scalar(0, 2)
-        drain_on_vector(0, 3)
-        catch_up(0)
-        multiply_all(LAST, 1)
-        for m in range(1, M_TILES):
-            catch_up(m)
-        for m in range(M_TILES):
-            drain_on_scalar(1, m)
-        prepare_alone(WHOLE, 2 * COLS, COLS, False)
-        multiply_all(WHOLE, 2)
-        g = LAST - 1
-        rows = load_columns(g, 2 * COLS, T)
-        first_half = load_columns(LAST, 2 * COLS, T - HALF)
-        rounded = chunk_pool.tile([P, COLS, PACK], BF16, name="chunk", tag="chunk", align_bytes=MX_ALIGN)
-        rounded_half = chunk_pool.tile([P, COLS, PACK], BF16, name="chunk", tag="chunk", align_bytes=MX_ALIGN)
-        own = COLS - SCALAR_SHARE[COLS]
-        round_and_interleave(nc.scalar.copy, rounded[:, own:, :], rows[:, :, own:])
-        round_and_interleave(nc.scalar.copy, rounded_half[:, P:HALF, :], first_half[:, :, P:])
-        round_and_interleave(nc.vector.tensor_copy, rounded[:, :HALF, :], rows[:, :, :HALF])
-        round_and_interleave(nc.vector.tensor_copy, rounded[:, HALF:own, :], rows[:, :, HALF:own])
-        new_codes(("x", g, 2))
-        new_codes(("x", LAST, 2))
-        quantise(("x", g, 2), 0, rounded[:, :HALF, :])
-        round_and_interleave(nc.vector.tensor_copy, rounded_half[:, :P, :], first_half[:, :, :P])
-        quantise(("x", g, 2), HALF, rounded[:, HALF:, :])
-        multiply_all(g, 2)
-        quantise(("x", LAST, 2), 0, rounded_half[:, :P, :])
-        quantise(("x", LAST, 2), P, rounded_half[:, P:HALF, :])
-        prepare_alone(LAST, T - HALF, HALF, True)
-        multiply_all(LAST, 2)
-        for m in range(M_TILES):
-            (add_on_vector if m in PARTIAL else drain_on_scalar)(2, m)
+        def reopen(key, bank, first):
+            open_bank(*key, bank)
+            for g in range(first, LAST - 1):
+                multiply(g, *key, False)
 
-        store(0, 2, 0, M_TILES // 2)
-        store(0, 2, M_TILES // 2, M_TILES)
-        store(2, T_TILES, 0, 1)
-        store(2, T_TILES, 1, M_TILES - 1)
-        store(2, T_TILES, M_TILES - 1, M_TILES)
+        def round_both(rows, c0, c1, share):
+            round_on(nc.scalar.copy, rows[0], rows[1], c1 - share, c1)
+            round_on(nc.vector.tensor_copy, rows[0], rows[1], c0, c1 - share)
+
+        for bank in range(len(twice)):
+            reopen(twice[bank], bank, PER + 1)
+        whole = ("B2", 1)
+        open_bank(*whole, len(twice))
+        for g in range(3):
+            multiply(g, *whole, False)
+
+        six = (new_chunk(), x6_late)
+        six_rest = (new_chunk(), x6_late[:, :, COLS:])
+        round_on(nc.vector.tensor_copy, *six, 0, HALF)
+        drain(True, "A2", 1)
+        round_on(nc.vector.tensor_copy, *six, HALF, COLS)
+        round_on(nc.scalar.copy, *six_rest, 0, HALF)
+        quantise("x", LAST - 1, EARLY, six[0], 0, HALF)
+        for i in range(2):
+            multiply(LAST - 1, "B0", i, False)
+        quantise("x", LAST - 1, EARLY, six[0], HALF, COLS)
+        for i in range(2):
+            multiply(LAST - 1, "B1", i, False)
+        multiply(3, *whole, False)
+
+        seven = (new_chunk(), x7_first)
+        round_on(nc.scalar.copy, *seven, P, HALF)
+        round_on(nc.vector.tensor_copy, *seven, 0, P)
+        round_both(seven, HALF, COLS, 96)
+        for c0 in (0, P):
+            quantise("x", LAST, EARLY, seven[0], c0, c0 + P)
+            for i in range(2):
+                multiply(LAST, "B0", i, c0 > 0, c0, c0 + P)
+        quantise("x", LAST, EARLY, seven[0], HALF, COLS)
+        for i in range(2):
+            multiply(LAST, "B1", i, True)
+        quantise("x", LAST - 1, EARLY + COLS, six_rest[0], 0, HALF)
+        for g in range(4, 6):
+            multiply(g, *whole, False)
+        for i in range(2):
+            multiply(LAST - 1, "B2", i, False)
+        eight = (new_chunk(), x7_second)
+        round_on(nc.scalar.copy, *eight, 0, P)
+        add("B0", 0)
+        drain(True, "B0", 1)
+        round_on(nc.vector.tensor_copy, *eight, P, HALF)
+        for c0 in (0, P):
+            quantise("x", LAST, EARLY + CUT, eight[0], c0, c0 + P)
+            for i in range(2):
+                multiply(LAST, "B2", i, c0 > 0, c0, c0 + P)
+        add("B1", 0)
+        drain(True, "B1", 1)
+        add("B2", 0)
+        drain(True, "B2", 1)
+
+        store(0, EARLY, 0, 1)
+        for span in ("B0", "B1", "B2"):
+            store(SPANS[span][0], SPANS[span][0] + HALF, 0, 1)

@@ -139,7 +139,7 @@ def tile_mix_jvp_fm_bias_kernel(tc, w, xd, wd, x, b, out):
             fresh[span, i] = True
 
         def rows_of(span, i):
-            return [i] if SPANS[span][1] == COLS else [2 * i, 2 * i + 1]
+            return [i] if SPANS[span][1] == COLS or i >= 2 else [2 * i, 2 * i + 1]
 
         def multiply(g, span, i, stop, c0=0, c1=None, only=None):
             col, width = SPANS[span]
@@ -171,17 +171,17 @@ def tile_mix_jvp_fm_bias_kernel(tc, w, xd, wd, x, b, out):
                 else:
                     nc.vector.tensor_scalar(out=dst, in0=src, scalar1=bias[:, m : m + 1], scalar2=None, op0=ADD)
 
-        def add(span, i):
+        def add(span, i, n0=0, n1=2):
             col, width = SPANS[span]
-            ms = rows_of(span, i)
-            part = res[:, ms[0] : ms[-1] + 1, col : col + width]
-            src = acc[span, i][:].rearrange("p (n c) -> p n c", c=width)
+            m = rows_of(span, i)[0]
+            part = res[:, m + n0 : m + n1, col : col + width]
+            src = acc[span, i][:].rearrange("p (n c) -> p n c", c=width)[:, n0:n1, :]
             nc.vector.tensor_tensor(out=part, in0=src, in1=part, op=ADD)
 
-        def store(c0, c1, m0, step):
+        def store(c0, c1, m0, m1):
             nc.sync.dma_start(
-                out=out[:, c0:c1].rearrange("(m p) c -> p m c", p=P)[:, m0::step, :],
-                in_=res[:, m0::step, c0:c1],
+                out=out[m0 * P : m1 * P, c0:c1].rearrange("(m p) c -> p m c", p=P),
+                in_=res[:, m0:m1, c0:c1],
             )
 
         xd_rows = load_passes(xd, 0, PER, X0)
@@ -269,55 +269,67 @@ def tile_mix_jvp_fm_bias_kernel(tc, w, xd, wd, x, b, out):
 
         for bank in range(len(twice)):
             reopen(twice[bank], bank, PER + 1)
-        whole = ("B2", 1)
-        open_bank(*whole, len(twice))
-        for g in range(3):
-            multiply(g, *whole, False)
+        whole = [("B2", 2), ("B2", 3)]
+        for n, key in enumerate(whole):
+            open_bank(*key, len(twice) + n)
+
+        def catch_up(g):
+            for key in whole:
+                multiply(g, *key, False)
+
+        for g in range(4):
+            catch_up(g)
 
         six = (new_chunk(), x6_late)
         six_rest = (new_chunk(), x6_late[:, :, COLS:])
         round_on(nc.vector.tensor_copy, *six, 0, HALF)
         drain(True, "A2", 1)
         round_on(nc.vector.tensor_copy, *six, HALF, COLS)
-        round_on(nc.scalar.copy, *six_rest, 0, HALF)
-        quantise("x", LAST - 1, EARLY, six[0], 0, HALF)
-        for i in range(2):
-            multiply(LAST - 1, "B0", i, False)
-        quantise("x", LAST - 1, EARLY, six[0], HALF, COLS)
-        for i in range(2):
-            multiply(LAST - 1, "B1", i, False)
-        multiply(3, *whole, False)
+        round_on(nc.scalar.copy, *six_rest, 0, P)
+        round_on(nc.scalar.copy, *six_rest, P, HALF)
+        for span in ("B0", "B1"):
+            c0 = SPANS[span][0] - EARLY
+            quantise("x", LAST - 1, EARLY, six[0], c0, c0 + HALF)
+            for i in range(2):
+                multiply(LAST - 1, span, i, False)
+        quantise("x", LAST - 1, EARLY + COLS, six_rest[0], 0, P)
+        catch_up(4)
 
         seven = (new_chunk(), x7_first)
-        round_on(nc.scalar.copy, *seven, P, HALF)
         round_on(nc.vector.tensor_copy, *seven, 0, P)
-        round_both(seven, HALF, COLS, 96)
+        round_both(seven, P, HALF, 96)
+        round_on(nc.scalar.copy, *seven, COLS - 160, COLS)
+        round_on(nc.vector.tensor_copy, *seven, HALF, HALF + 64)
         for c0 in (0, P):
             quantise("x", LAST, EARLY, seven[0], c0, c0 + P)
             for i in range(2):
                 multiply(LAST, "B0", i, c0 > 0, c0, c0 + P)
-        quantise("x", LAST, EARLY, seven[0], HALF, COLS)
-        for i in range(2):
-            multiply(LAST, "B1", i, True)
-        quantise("x", LAST - 1, EARLY + COLS, six_rest[0], 0, HALF)
-        for g in range(4, 6):
-            multiply(g, *whole, False)
-        for i in range(2):
-            multiply(LAST - 1, "B2", i, False)
+        round_on(nc.vector.tensor_copy, *seven, HALF + 64, COLS - 160)
+        quantise("x", LAST - 1, EARLY + COLS, six_rest[0], P, HALF)
         eight = (new_chunk(), x7_second)
-        round_on(nc.scalar.copy, *eight, 0, P)
+        round_both(eight, 0, HALF, P)
+        quantise("x", LAST, EARLY, seven[0], HALF, COLS)
+        catch_up(5)
+        multiply(LAST - 1, *whole[0], False)
+        for i in (1, 0):
+            multiply(LAST, "B1", i, True)
+        multiply(LAST - 1, *whole[1], False)
         add("B0", 0)
         drain(True, "B0", 1)
-        round_on(nc.vector.tensor_copy, *eight, P, HALF)
+        drain(True, "B1", 1)
         for c0 in (0, P):
             quantise("x", LAST, EARLY + CUT, eight[0], c0, c0 + P)
-            for i in range(2):
-                multiply(LAST, "B2", i, c0 > 0, c0, c0 + P)
-        add("B1", 0)
-        drain(True, "B1", 1)
+            for key in whole:
+                multiply(LAST, *key, c0 > 0, c0, c0 + P)
+        multiply(LAST - 1, "B2", 0, False)
+        multiply(LAST, "B2", 0, True)
+        add("B1", 0, 0, 1)
+        drain(True, "B2", 2)
+        drain(False, "B2", 3)
+        add("B1", 0, 1, 2)
         add("B2", 0)
-        drain(True, "B2", 1)
 
-        store(0, EARLY, 0, 1)
-        for span in ("B0", "B1", "B2"):
-            store(SPANS[span][0], SPANS[span][0] + HALF, 0, 1)
+        store(0, EARLY, 0, M_TILES)
+        store(EARLY, EARLY + HALF, 0, M_TILES)
+        store(EARLY + HALF, T, 2, M_TILES)
+        store(EARLY + HALF, T, 0, 2)

@@ -85,7 +85,7 @@ def tile_mix_jvp_fm_bias_kernel(tc, w, xd, wd, x, b, out):
                 if c0 < COLS:
                     key = ("first", g)
                     if key not in codes_of:
-                        new_codes(key, COLS, "first%d" % (g if g <= PER + 1 else g - PER))
+                        new_codes(key, COLS, "first%d" % (g % LAST))
                 elif c0 >= T - HALF:
                     key = ("end", g)
                     c0 = c0 - (T - HALF)
@@ -116,7 +116,7 @@ def tile_mix_jvp_fm_bias_kernel(tc, w, xd, wd, x, b, out):
             codes, scales = operand(kind, g, col + c0, c1 - c0)
             nc.vector.quantize_mx(out=codes, scales=scales, in_=rounded[:, c0:c1, :].rearrange("p c j -> p (c j)"))
 
-        def prepare(chunks):
+        def prepare(chunks, after=None):
             waiting = None
             for kind, g, col, rows in chunks:
                 width = rows.shape[2]
@@ -125,6 +125,8 @@ def tile_mix_jvp_fm_bias_kernel(tc, w, xd, wd, x, b, out):
                 round_on(nc.vector.tensor_copy, rounded, rows, width // 2, width)
                 if waiting is not None:
                     quantise(*waiting[:4], 0, waiting[4])
+                    if after and waiting[:3] in after:
+                        after[waiting[:3]]()
                 waiting = (kind, g, col, rounded, width)
             width = waiting[4]
             quantise(*waiting[:4], width // 2, width)
@@ -218,25 +220,58 @@ def tile_mix_jvp_fm_bias_kernel(tc, w, xd, wd, x, b, out):
         for g in range(PER):
             for key in twice + stay:
                 multiply(g, *key, False)
-        prepare([("w", PER + i, 0, wd_rows[i]) for i in range(PER - 1)])
-        prepare(x_chunks(PER, x4_rows, 0)[::-1])
-        for key in reversed(twice):
-            multiply(PER, *key, True)
-        for key in reversed(stay):
-            multiply(PER, *key, False)
-        for bank in reversed(range(len(twice))):
-            drain(True, *twice[bank])
-            open_bank("A", bank, bank)
-            for g in range(PER + 1):
-                multiply(g, "A", bank, False)
         moved = [("A", m) for m in range(len(twice))]
+
+        def fifth_pass(keys):
+            for key in keys:
+                multiply(PER, *key, key in twice[1:])
+
+        def hand_over(bank, passes):
+            drain(True, *twice[bank])
+            open_bank(*moved[bank], bank)
+            for g in range(passes):
+                multiply(g, *moved[bank], False)
+
+        wd_chunks = [("w", PER + i, 0, wd_rows[i]) for i in range(PER - 1)]
+        prepare(
+            wd_chunks[:2] + x_chunks(PER, x4_rows, 0)[::-1] + wd_chunks[2:],
+            {
+                ("x", PER, 2 * COLS): lambda: fifth_pass([("B2", 0), ("B1", 0), ("B1", 1)]),
+                ("x", PER, COLS): lambda: fifth_pass([("B0", 0), ("B0", 1), ("A2", 0), ("A2", 1)]),
+                ("x", PER, 0): lambda: fifth_pass([("A", 3)]),
+            },
+        )
+        for bank in (2, 1):
+            hand_over(bank, PER + 1)
         prepare(x_chunks(PER + 1, x5_rows, 0))
-        for key in moved + stay:
-            multiply(PER + 1, *key, False)
-        prepare(x_chunks(LAST - 1, x6_early, 0))
-        for key in moved + stay[:3]:
-            multiply(LAST - 1, *key, False)
-        prepare(x_chunks(LAST, x7_early, 0))
+        for key in moved[1:] + stay[:1] + twice[:1] + stay[1:]:
+            multiply(PER + 1, *key, key == twice[0])
+
+        def round_both(rows, c0, c1, share):
+            round_on(nc.scalar.copy, rows[0], rows[1], c1 - share, c1)
+            round_on(nc.vector.tensor_copy, rows[0], rows[1], c0, c1 - share)
+
+        early = {}
+        a_banks = moved + stay[:1]
+        for g, rows in ((LAST - 1, x6_early), (LAST, x7_early)):
+            early[g] = ((new_chunk(), rows), (new_chunk(), rows[:, :, COLS:]))
+            round_both(early[g][0], 0, COLS, HALF)
+            round_both(early[g][1], 0, HALF, P)
+            if g < LAST:
+                quantise("x", g, 0, early[g][0][0], 0, HALF)
+                for key in a_banks[1:]:
+                    multiply(g, *key, False, 0, HALF)
+                hand_over(0, g)
+                multiply(g, *a_banks[0], False, 0, HALF)
+        g = LAST - 1
+        quantise("x", g, 0, early[g][0][0], HALF, COLS)
+        quantise("x", g, COLS, early[g][1][0], 0, HALF)
+        for key in a_banks:
+            multiply(g, *key, False, HALF, COLS)
+        for key in stay[1:3]:
+            multiply(g, *key, False)
+        quantise("x", LAST, 0, early[LAST][0][0], 0, COLS)
+        quantise("x", LAST, COLS, early[LAST][1][0], 0, HALF)
 
         rounded = new_chunk()
 
@@ -258,27 +293,20 @@ def tile_mix_jvp_fm_bias_kernel(tc, w, xd, wd, x, b, out):
         drain(False, "A", 2)
         drain(True, "A", 3)
 
-        def reopen(key, bank, first):
-            open_bank(*key, bank)
-            for g in range(first, LAST - 1):
-                multiply(g, *key, False)
-
-        def round_both(rows, c0, c1, share):
-            round_on(nc.scalar.copy, rows[0], rows[1], c1 - share, c1)
-            round_on(nc.vector.tensor_copy, rows[0], rows[1], c0, c1 - share)
-
-        for bank in range(len(twice)):
-            reopen(twice[bank], bank, PER + 1)
         whole = [("B2", 2), ("B2", 3)]
-        for n, key in enumerate(whole):
-            open_bank(*key, len(twice) + n)
+        for bank, key in enumerate(whole):
+            open_bank(*key, bank)
 
         def catch_up(g):
             for key in whole:
                 multiply(g, *key, False)
 
-        for g in range(4):
+        for g in range(PER + 1):
             catch_up(g)
+        for key, bank in ((twice[1], 4), (twice[2], 2)):
+            open_bank(*key, bank)
+            multiply(PER + 1, *key, False)
+        open_bank(*twice[0], 3)
 
         six = (new_chunk(), x6_late)
         six_rest = (new_chunk(), x6_late[:, :, COLS:])
@@ -293,7 +321,6 @@ def tile_mix_jvp_fm_bias_kernel(tc, w, xd, wd, x, b, out):
             for i in range(2):
                 multiply(LAST - 1, span, i, False)
         quantise("x", LAST - 1, EARLY + COLS, six_rest[0], 0, P)
-        catch_up(4)
 
         seven = (new_chunk(), x7_first)
         round_on(nc.vector.tensor_copy, *seven, 0, P)

@@ -213,18 +213,18 @@ def tile_mix_jvp_fm_bias_kernel(tc, w, xd, wd, x, b, out):
         x7_first = load_columns(LAST, EARLY, EARLY + CUT, late + PACK * EARLY)
         x7_second = load_columns(LAST, EARLY + CUT, T, late + PACK * (EARLY + CUT))
 
-        twice = [("B0", 0), ("B1", 0), ("B2", 0)]
-        stay = [("A", 3), ("A2", 0), ("A2", 1), ("B0", 1), ("B1", 1)]
+        twice = [("B0", 0), ("B1", 0), ("B2", 0), ("B2", 3)]
+        stay = [("A2", 0), ("A2", 1), ("B0", 1), ("B1", 1)]
         for bank, key in enumerate(twice + stay):
             open_bank(*key, bank)
         for g in range(PER):
-            for key in twice + stay:
-                multiply(g, *key, False)
-        moved = [("A", m) for m in range(len(twice))]
+            for key in twice[::-1] + stay:
+                multiply(g, *key, key == twice[3] and g == PER - 1)
+        moved = [("A", m) for m in range(M_TILES)]
 
         def fifth_pass(keys):
             for key in keys:
-                multiply(PER, *key, key in twice[1:])
+                multiply(PER, *key, key in twice[1:3])
 
         def hand_over(bank, passes):
             drain(True, *twice[bank])
@@ -236,6 +236,7 @@ def tile_mix_jvp_fm_bias_kernel(tc, w, xd, wd, x, b, out):
         prepare(
             wd_chunks[:2] + x_chunks(PER, x4_rows, 0)[::-1] + wd_chunks[2:],
             {
+                ("w", PER, 0): lambda: hand_over(3, PER),
                 ("x", PER, 2 * COLS): lambda: fifth_pass([("B2", 0), ("B1", 0), ("B1", 1)]),
                 ("x", PER, COLS): lambda: fifth_pass([("B0", 0), ("B0", 1), ("A2", 0), ("A2", 1)]),
                 ("x", PER, 0): lambda: fifth_pass([("A", 3)]),
@@ -244,7 +245,7 @@ def tile_mix_jvp_fm_bias_kernel(tc, w, xd, wd, x, b, out):
         for bank in (2, 1):
             hand_over(bank, PER + 1)
         prepare(x_chunks(PER + 1, x5_rows, 0))
-        for key in moved[1:] + stay[:1] + twice[:1] + stay[1:]:
+        for key in moved[1:] + twice[:1] + stay:
             multiply(PER + 1, *key, key == twice[0])
 
         def round_both(rows, c0, c1, share):
@@ -252,23 +253,22 @@ def tile_mix_jvp_fm_bias_kernel(tc, w, xd, wd, x, b, out):
             round_on(nc.vector.tensor_copy, rows[0], rows[1], c0, c1 - share)
 
         early = {}
-        a_banks = moved + stay[:1]
         for g, rows in ((LAST - 1, x6_early), (LAST, x7_early)):
             early[g] = ((new_chunk(), rows), (new_chunk(), rows[:, :, COLS:]))
             round_both(early[g][0], 0, COLS, HALF)
             round_both(early[g][1], 0, HALF, P)
             if g < LAST:
                 quantise("x", g, 0, early[g][0][0], 0, HALF)
-                for key in a_banks[1:]:
+                for key in moved[1:]:
                     multiply(g, *key, False, 0, HALF)
                 hand_over(0, g)
-                multiply(g, *a_banks[0], False, 0, HALF)
+                multiply(g, *moved[0], False, 0, HALF)
         g = LAST - 1
         quantise("x", g, 0, early[g][0][0], HALF, COLS)
         quantise("x", g, COLS, early[g][1][0], 0, HALF)
-        for key in a_banks:
+        for key in moved:
             multiply(g, *key, False, HALF, COLS)
-        for key in stay[1:3]:
+        for key in stay[:2]:
             multiply(g, *key, False)
         quantise("x", LAST, 0, early[LAST][0][0], 0, COLS)
         quantise("x", LAST, COLS, early[LAST][1][0], 0, HALF)
@@ -301,7 +301,9 @@ def tile_mix_jvp_fm_bias_kernel(tc, w, xd, wd, x, b, out):
             for key in whole:
                 multiply(g, *key, False)
 
-        for g in range(PER + 1):
+        for g in range(PER):
+            multiply(g, *whole[0], False)
+        for g in (PER, PER + 1):
             catch_up(g)
         for key, bank in ((twice[1], 4), (twice[2], 2)):
             open_bank(*key, bank)
@@ -336,23 +338,22 @@ def tile_mix_jvp_fm_bias_kernel(tc, w, xd, wd, x, b, out):
         eight = (new_chunk(), x7_second)
         round_both(eight, 0, HALF, P)
         quantise("x", LAST, EARLY, seven[0], HALF, COLS)
-        catch_up(5)
-        multiply(LAST - 1, *whole[0], False)
+        catch_up(LAST - 1)
         for i in (1, 0):
             multiply(LAST, "B1", i, True)
-        multiply(LAST - 1, *whole[1], False)
+        multiply(LAST - 1, "B2", 0, False, only=0)
         add("B0", 0)
         drain(True, "B0", 1)
         drain(True, "B1", 1)
         for c0 in (0, P):
             quantise("x", LAST, EARLY + CUT, eight[0], c0, c0 + P)
-            for key in whole:
+            for key in reversed(whole):
                 multiply(LAST, *key, c0 > 0, c0, c0 + P)
-        multiply(LAST - 1, "B2", 0, False)
+        multiply(LAST - 1, "B2", 0, False, only=1)
         multiply(LAST, "B2", 0, True)
         add("B1", 0, 0, 1)
         drain(True, "B2", 2)
-        drain(False, "B2", 3)
+        add("B2", 3, 0, 1)
         add("B1", 0, 1, 2)
         add("B2", 0)
 

from contextlib import ExitStack

import concourse.mybir as mybir
from concourse.masks import make_identity

K, M, T = 2048, 512, 1536
FLOPS = 2 * 2 * K * M * T

F32 = mybir.dt.float32
BF16 = mybir.dt.bfloat16
U32 = mybir.dt.uint32
U8 = mybir.dt.uint8
E4M3 = mybir.dt.float8_e4m3fn_x4
E5M2 = mybir.dt.float8_e5m2_x4
ADD = mybir.AluOpType.add
IDENTITY = mybir.ActivationFunctionType.Identity

P = 128
PACK = 4
K_PASS = P * PACK
COLS = 512
HALF = COLS // 2
PER = K // K_PASS
LAST = 2 * PER - 1
M_TILES = M // P
RUN = 4
MX_ALIGN = 64
DMA_ALIGN = 256

SPANS = {"A": (0, COLS), "A2": (COLS, HALF), "B0": (3 * HALF, HALF), "B1": (4 * HALF, HALF), "B2": (5 * HALF, HALF)}
EARLY = COLS + HALF
X_SLOT = PACK * T
W_SLOT = PACK * M
X0 = 0
W0 = X0 + PER * X_SLOT
STAGE = W0 + PER * W_SLOT
AHEAD = 7
CUT = COLS


def tile_mix_jvp_fm_bias_kernel(tc, w, xd, wd, x, b, out):
    nc = tc.nc

    with ExitStack() as ctx:
        stage_pool = ctx.enter_context(tc.tile_pool(name="stage", bufs=1))
        chunk_pool = ctx.enter_context(tc.tile_pool(name="chunks", bufs=4))
        keep = ctx.enter_context(tc.tile_pool(name="keep", bufs=1))
        psum = ctx.enter_context(tc.psum_pool(name="psum", bufs=1))
        ctx.enter_context(tc.manual_schedule())

        stage = stage_pool.tile([P, STAGE], F32, name="stage", tag="stage", align_bytes=DMA_ALIGN)
        res = stage_pool.tile([P, M_TILES, T], F32, name="res", tag="res", align_bytes=DMA_ALIGN)

        codes_of = {}
        acc = {}
        fresh = {}

        def load_passes(src, first, count, at):
            width = src.shape[1]
            rows = stage[:, at : at + count * PACK * width].rearrange("p (g r) -> p g r", g=count)
            nc.sync.dma_start(
                out=rows,
                in_=src[first * K_PASS : (first + count) * K_PASS, :].rearrange("(g p j) c -> p g (j c)", g=count, j=PACK),
            )
            return [rows[:, g, :].rearrange("p (j c) -> p j c", j=PACK) for g in range(count)]

        def load_columns(g, c0, c1, at):
            k0 = (g - PER) * K_PASS
            rows = stage[:, at : at + PACK * (c1 - c0)].rearrange("p (j c) -> p j c", j=PACK)
            nc.sync.dma_start(out=rows, in_=x[k0 : k0 + K_PASS, c0:c1].rearrange("(p j) c -> p j c", j=PACK))
            return rows

        def new_codes(key, width, label):
            codes = keep.tile([P, width], U32, name="codes_" + label, tag="codes_" + label, align_bytes=MX_ALIGN)
            scales = keep.tile([P, width], U8, name="scales_" + label, tag="scales_" + label, align_bytes=MX_ALIGN)
            codes_of[key] = (codes, scales)

        def operand(kind, g, c0, width):
            if kind == "w":
                key, fmt = ("w", g), (E4M3 if g < PER else E5M2)
                if key not in codes_of:
                    new_codes(key, M, "w%d" % g)
            else:
                fmt = E5M2 if g < PER else E4M3
                if c0 < COLS:
                    key = ("first", g)
                    if key not in codes_of:
                        new_codes(key, COLS, "first%d" % (g % LAST))
                elif c0 >= T - HALF:
                    key = ("end", g)
                    c0 = c0 - (T - HALF)
                    if key not in codes_of:
                        new_codes(key, HALF, "end%d" % g)
                else:
                    key = ("rest", g)
                    c0 = c0 - COLS
                    if key not in codes_of:
                        new_codes(key, T - COLS - HALF, "rest%d" % (g % PER))
            codes, scales = codes_of[key]
            return codes[:, c0 : c0 + width].bitcast(fmt), scales[:, c0 : c0 + width]

        def new_chunk():
            return chunk_pool.tile([P, COLS, PACK], BF16, name="chunk", tag="chunk", align_bytes=MX_ALIGN)

        def round_on(copy, rounded, rows, c0, c1):
            copy(
                out=rounded[:, c0:c1, :].rearrange("p (c i) j -> p c j i", i=RUN),
                in_=rows[:, :, c0:c1].rearrange("p j (c i) -> p c j i", i=RUN),
            )

        def quantise(kind, g, col, rounded, c0, c1):
            if kind == "x" and col + c0 < T - HALF < col + c1:
                quantise(kind, g, col, rounded, c0, T - HALF - col)
                quantise(kind, g, col, rounded, T - HALF - col, c1)
                return
            codes, scales = operand(kind, g, col + c0, c1 - c0)
            nc.vector.quantize_mx(out=codes, scales=scales, in_=rounded[:, c0:c1, :].rearrange("p c j -> p (c j)"))

        def prepare(chunks, after=None):
            waiting = None
            for kind, g, col, rows in chunks:
                width = rows.shape[2]
                rounded = new_chunk()
                round_on(nc.scalar.copy, rounded, rows, 0, width // 2)
                round_on(nc.vector.tensor_copy, rounded, rows, width // 2, width)
                if waiting is not None:
                    quantise(*waiting[:4], 0, waiting[4])
                    if after and waiting[:3] in after:
                        after[waiting[:3]]()
                waiting = (kind, g, col, rounded, width)
            width = waiting[4]
            quantise(*waiting[:4], width // 2, width)
            quantise(*waiting[:4], 0, width // 2)

        def x_chunks(g, rows, col):
            width = rows.shape[2]
            return [("x", g, col + c, rows[:, :, c : min(c + COLS, width)]) for c in range(0, width, COLS)]

        def open_bank(span, i, bank):
            acc[span, i] = psum.tile([P, COLS], F32, name="bank%d" % bank, tag="bank%d" % bank)
            fresh[span, i] = True

        def rows_of(span, i):
            return [i] if SPANS[span][1] == COLS or i >= 2 else [2 * i, 2 * i + 1]

        def multiply(g, span, i, stop, c0=0, c1=None, only=None):
            col, width = SPANS[span]
            c1 = width if c1 is None else c1
            ms = rows_of(span, i)
            for n, m in enumerate(ms):
                if only is not None and m != only:
                    continue
                w_codes, w_scales = operand("w", g, m * P, P)
                x_codes, x_scales = operand("x", g, col + c0, c1 - c0)
                nc.tensor.matmul_mx(
                    out=acc[span, i][:, n * width + c0 : n * width + c1],
                    lhsT=w_codes,
                    lhsT_scale=w_scales,
                    rhs=x_codes,
                    rhs_scale=x_scales,
                    start=fresh[span, i],
                    stop=(stop and m == ms[-1]),
                )
                fresh[span, i] = False

        def drain(on_scalar, span, i):
            col, width = SPANS[span]
            for n, m in enumerate(rows_of(span, i)):
                dst = res[:, m, col : col + width]
                src = acc[span, i][:, n * width : (n + 1) * width]
                if on_scalar:
                    nc.scalar.activation(out=dst, in_=src, func=IDENTITY, bias=bias[:, m : m + 1])
                else:
                    nc.vector.tensor_scalar(out=dst, in0=src, scalar1=bias[:, m : m + 1], scalar2=None, op0=ADD)

        def add(span, i, n0=0, n1=2):
            col, width = SPANS[span]
            m = rows_of(span, i)[0]
            part = res[:, m + n0 : m + n1, col : col + width]
            src = acc[span, i][:].rearrange("p (n c) -> p n c", c=width)[:, n0:n1, :]
            nc.vector.tensor_tensor(out=part, in0=src, in1=part, op=ADD)

        def store(c0, c1, m0, m1):
            nc.sync.dma_start(
                out=out[m0 * P : m1 * P, c0:c1].rearrange("(m p) c -> p m c", p=P),
                in_=res[:, m0:m1, c0:c1],
            )

        xd_rows = load_passes(xd, 0, PER, X0)
        b_rows = keep.tile([P, P], F32, name="b_rows", tag="b_rows")
        ident = keep.tile([P, P], F32, name="ident", tag="ident")
        bias = keep.tile([P, M_TILES], F32, name="bias", tag="bias")
        nc.vector.memset(b_rows[:], 0.0)
        nc.sync.dma_start(out=b_rows[:M_TILES, :], in_=b.rearrange("(m p) -> m p", p=P))
        make_identity(nc, ident[:])
        w_rows = load_passes(w, 0, PER, W0)
        b_cols = psum.tile([P, P], F32, name="b_cols", tag="bank7")
        nc.tensor.transpose(b_cols[:], b_rows[:], ident[:])
        nc.scalar.activation(out=bias[:], in_=b_cols[:, :M_TILES], func=IDENTITY)

        xd_chunks = [c for g in range(PER) for c in x_chunks(g, xd_rows[g], 0)]
        prepare(xd_chunks[:AHEAD])
        wd_rows = load_passes(wd, 0, PER - 1, X0)
        x4_rows = load_passes(x, 0, 1, X0 + X_SLOT)[0]
        prepare([("w", g, 0, w_rows[g]) for g in range(PER)])
        prepare(xd_chunks[AHEAD:])
        x5_rows = load_passes(x, 1, 1, X0 + 2 * X_SLOT)[0]
        x6_early = load_columns(LAST - 1, 0, EARLY, W0)
        x7_early = load_columns(LAST, 0, EARLY, W0 + PACK * EARLY)
        w7_rows = load_passes(wd, PER - 1, 1, W0 + 2 * PACK * EARLY)[0]
        late = X0 + 3 * X_SLOT
        x6_late = load_columns(LAST - 1, EARLY, T, late)
        x7_first = load_columns(LAST, EARLY, EARLY + CUT, late + PACK * EARLY)
        x7_second = load_columns(LAST, EARLY + CUT, T, late + PACK * (EARLY + CUT))

        twice = [("B0", 0), ("B1", 0), ("B2", 0), ("B2", 3)]
        stay = [("A2", 0), ("A2", 1), ("B0", 1), ("B1", 1)]
        for bank, key in enumerate(twice + stay):
            open_bank(*key, bank)
        for g in range(PER):
            for key in twice[::-1] + stay:
                multiply(g, *key, key == twice[3] and g == PER - 1)
        moved = [("A", m) for m in range(M_TILES)]

        def fifth_pass(keys):
            for key in keys:
                multiply(PER, *key, key in twice[1:3])

        def hand_over(bank, passes):
            drain(True, *twice[bank])
            open_bank(*moved[bank], bank)
            for g in range(passes):
                multiply(g, *moved[bank], False)

        wd_chunks = [("w", PER + i, 0, wd_rows[i]) for i in range(PER - 1)]
        prepare(
            wd_chunks[:2] + x_chunks(PER, x4_rows, 0)[::-1] + wd_chunks[2:],
            {
                ("w", PER, 0): lambda: hand_over(3, PER),
                ("x", PER, 2 * COLS): lambda: fifth_pass([("B2", 0), ("B1", 0), ("B1", 1)]),
                ("x", PER, COLS): lambda: fifth_pass([("B0", 0), ("B0", 1), ("A2", 0), ("A2", 1)]),
                ("x", PER, 0): lambda: fifth_pass([("A", 3)]),
            },
        )
        for bank in (2, 1):
            hand_over(bank, PER + 1)
        prepare(x_chunks(PER + 1, x5_rows, 0))
        for key in moved[1:] + twice[:1] + stay:
            multiply(PER + 1, *key, key == twice[0])

        def round_both(rows, c0, c1, share):
            round_on(nc.scalar.copy, rows[0], rows[1], c1 - share, c1)
            round_on(nc.vector.tensor_copy, rows[0], rows[1], c0, c1 - share)

        early = {}
        for g, rows in ((LAST - 1, x6_early), (LAST, x7_early)):
            early[g] = ((new_chunk(), rows), (new_chunk(), rows[:, :, COLS:]))
            round_both(early[g][0], 0, COLS, HALF)
            round_both(early[g][1], 0, HALF, P)
            if g < LAST:
                quantise("x", g, 0, early[g][0][0], 0, HALF)
                for key in moved[1:]:
                    multiply(g, *key, False, 0, HALF)
                hand_over(0, g)
                multiply(g, *moved[0], False, 0, HALF)
        g = LAST - 1
        quantise("x", g, 0, early[g][0][0], HALF, COLS)
        quantise("x", g, COLS, early[g][1][0], 0, HALF)
        for key in moved:
            multiply(g, *key, False, HALF, COLS)
        for key in stay[:2]:
            multiply(g, *key, False)
        quantise("x", LAST, 0, early[LAST][0][0], 0, COLS)
        quantise("x", LAST, COLS, early[LAST][1][0], 0, HALF)

        rounded = new_chunk()

        def close_rows(m):
            quantise("w", LAST, 0, rounded, m * P, (m + 1) * P)
            multiply(LAST, "A", m, True)
            multiply(LAST, "A2", m // 2, True, only=m)

        round_on(nc.scalar.copy, rounded, w7_rows, 2 * P, 3 * P)
        round_on(nc.vector.tensor_copy, rounded, w7_rows, 0, P)
        round_on(nc.vector.tensor_copy, rounded, w7_rows, P, 2 * P)
        close_rows(0)
        round_on(nc.vector.tensor_copy, rounded, w7_rows, 3 * P, 4 * P)
        for m in range(1, M_TILES):
            close_rows(m)
        drain(True, "A", 0)
        drain(False, "A", 1)
        drain(True, "A2", 0)
        drain(False, "A", 2)
        drain(True, "A", 3)

        whole = [("B2", 2), ("B2", 3)]
        for bank, key in enumerate(whole):
            open_bank(*key, bank)

        def catch_up(g):
            for key in whole:
                multiply(g, *key, False)

        for g in range(PER):
            multiply(g, *whole[0], False)
        for g in (PER, PER + 1):
            catch_up(g)
        for key, bank in ((twice[1], 4), (twice[2], 2)):
            open_bank(*key, bank)
            multiply(PER + 1, *key, False)
        open_bank(*twice[0], 3)

        six = (new_chunk(), x6_late)
        six_rest = (new_chunk(), x6_late[:, :, COLS:])
        round_on(nc.vector.tensor_copy, *six, 0, HALF)
        drain(True, "A2", 1)
        round_on(nc.vector.tensor_copy, *six, HALF, COLS)
        round_on(nc.scalar.copy, *six_rest, 0, P)
        round_on(nc.scalar.copy, *six_rest, P, HALF)
        for span in ("B0", "B1"):
            c0 = SPANS[span][0] - EARLY
            quantise("x", LAST - 1, EARLY, six[0], c0, c0 + HALF)
            for i in range(2):
                multiply(LAST - 1, span, i, False)
        quantise("x", LAST - 1, EARLY + COLS, six_rest[0], 0, P)

        seven = (new_chunk(), x7_first)
        round_on(nc.vector.tensor_copy, *seven, 0, P)
        round_both(seven, P, HALF, 96)
        round_on(nc.scalar.copy, *seven, COLS - 160, COLS)
        round_on(nc.vector.tensor_copy, *seven, HALF, HALF + 64)
        for c0 in (0, P):
            quantise("x", LAST, EARLY, seven[0], c0, c0 + P)
            for i in range(2):
                multiply(LAST, "B0", i, c0 > 0, c0, c0 + P)
        round_on(nc.vector.tensor_copy, *seven, HALF + 64, COLS - 160)
        quantise("x", LAST - 1, EARLY + COLS, six_rest[0], P, HALF)
        eight = (new_chunk(), x7_second)
        round_both(eight, 0, HALF, P)
        quantise("x", LAST, EARLY, seven[0], HALF, COLS)
        catch_up(LAST - 1)
        for i in (1, 0):
            multiply(LAST, "B1", i, True)
        multiply(LAST - 1, "B2", 0, False, only=0)
        add("B0", 0)
        drain(True, "B0", 1)
        drain(True, "B1", 1)
        for c0 in (0, P):
            quantise("x", LAST, EARLY + CUT, eight[0], c0, c0 + P)
            for key in reversed(whole):
                multiply(LAST, *key, c0 > 0, c0, c0 + P)
        multiply(LAST - 1, "B2", 0, False, only=1)
        multiply(LAST, "B2", 0, True)
        add("B1", 0, 0, 1)
        drain(True, "B2", 2)
        add("B2", 3, 0, 1)
        add("B1", 0, 1, 2)
        add("B2", 0)

        store(0, EARLY, 0, M_TILES)
        store(EARLY, EARLY + HALF, 0, M_TILES)
        store(EARLY + HALF, T, 2, M_TILES)
        store(EARLY + HALF, T, 0, 2)
